import numpy as np
import ml_dtypes


def mxq(x, axis, fmt="e4m3"):
    dtype, down = {"e4m3": (ml_dtypes.float8_e4m3fn, 7), "e5m2": (ml_dtypes.float8_e5m2, 14)}[fmt]
    v = np.moveaxis(np.asarray(x, np.float32).astype(ml_dtypes.bfloat16).astype(np.float64), axis, -1)
    blocks = v.reshape(v.shape[:-1] + (-1, 32))
    amax = np.abs(blocks).max(-1, keepdims=True)
    byte = np.maximum(np.where(amax > 0, np.frexp(amax)[1] - 1 + 127, 0) - down, 1)
    scale = np.exp2(byte - 127.0)
    codes = (blocks / scale).astype(np.float32).astype(dtype).astype(np.float64)
    return np.moveaxis((codes * scale).reshape(v.shape), -1, axis)


WIDE = False


def mx_kscale(k):
    if not WIDE:
        return np.ones(k)
    levels = np.array([10, -10, 5, -5, 0])
    if k % 512:
        return np.exp2(np.random.permutation(np.resize(levels, k // 32))).repeat(32)
    a = np.empty((k // 512, 16))
    for p in range(k // 512):
        a[p, :8] = np.random.permutation(np.resize(levels, 8))
        for g in range(8):
            far = levels[np.abs(levels - a[p, g]) >= 10]
            a[p, g + 8] = far[np.random.randint(len(far))]
    return np.exp2(a.ravel()).repeat(32)


BF16 = ml_dtypes.bfloat16


def bf(x):
    return np.asarray(x, np.float32).astype(BF16)


def f64(x):
    return np.asarray(x).astype(np.float64)


N, D, V, E = 512, 1024, 2048, 1024


def scaled_softmax(logits):
    vocab = logits.shape[-1]
    e = np.exp(logits - logits.max(-1, keepdims=True))
    return vocab * (e / e.sum(-1, keepdims=True))


def residual(p, q):
    d = np.maximum(p - q, 0.0)
    return d / d.mean(-1, keepdims=True)


def draw0():
    s, t = mx_kscale(D), mx_kscale(V)
    return {
        "h_t": bf(np.random.standard_normal((N, D)) * s),
        "w_t": bf(np.random.standard_normal((D, V)) / np.sqrt(D) / s[:, None]),
        "q1": bf(np.random.uniform(0.0, 2.0, (N, V))),
        "q2": bf(np.random.uniform(0.0, 2.0, (N, V))),
        "g": bf(np.random.standard_normal(V) * t),
        "emb": bf(np.random.standard_normal((V, E)) / np.sqrt(V) / t[:, None]),
    }


def core(h_t, w_t, q1, q2, g, emb):
    lt = mxq(f64(h_t), 1, "e4m3") @ mxq(f64(w_t), 0, "e4m3")
    p = scaled_softmax(lt)
    r1 = residual(p, f64(q1))
    r2 = residual(r1, f64(q2))
    c = r2 * f64(g)[None, :]
    return mxq(c, 1, "e4m3") @ mxq(f64(emb), 0, "e4m3")


def e4m3fn_bytes(y):
    return np.clip(np.asarray(y, np.float64), -448.0, 448.0).astype(np.float32).astype(ml_dtypes.float8_e4m3fn).view(np.uint8)


def e4m3fn_values(b):
    return np.asarray(b, np.uint8).view(ml_dtypes.float8_e4m3fn).astype(np.float64)


def setup_inputs():
    d = draw0()
    x0 = np.asarray(d['w_t']).astype(np.float64)
    s = (np.max(np.abs(x0), axis=(1,), keepdims=True) / 448.0).astype(np.float32)
    out = {}
    for k, v in d.items():
        if k == 'w_t':
            out['w_t_bytes'] = e4m3fn_bytes(x0 / s.astype(np.float64))
            out['w_t_scale'] = s
        else:
            out[k] = v
    return out


def reference(h_t, w_t_bytes, w_t_scale, q1, q2, g, emb):
    return core(h_t, e4m3fn_values(w_t_bytes) * w_t_scale.astype(np.float64), q1, q2, g, emb)

@@ -1,0 +1,352 @@
+from contextlib import ExitStack
+
+import concourse.mybir as mybir
+from concourse.masks import make_identity
+
+F32 = mybir.dt.float32
+BF16 = mybir.dt.bfloat16
+U32 = mybir.dt.uint32
+U8 = mybir.dt.uint8
+F8 = mybir.dt.float8_e4m3fn
+F8X4 = mybir.dt.float8_e4m3fn_x4
+ACT = mybir.ActivationFunctionType
+ALU = mybir.AluOpType
+AX = mybir.AxisListType
+
+N, D, V, E = 512, 1024, 2048, 1024
+P = 128
+PACK = 4
+FLOPS = 2 * N * D * V + 2 * N * V * E
+TILES = N // P
+CH = 512
+INV_V = 1.0 / V
+
+ORDER = """
+W:0 I:0 W:2 W:3 I:2 Q:0 W:1 W:6 I:3 hc:0 I:1 hc:1 W:4 Q:1
+I:6 W:5 Q:6 I:4 qh:0 EI:1 I:5 Q:4 Q:3 W:7 m:0.0 Q:5 EQ:1 Q:2
+EI:0 I:7 Q:7 m:0.1 hc:2 m:0.2 EI:2 m:0.3 EI:5 n:0 EQ:0 e:0.0 EI:3 e:0.1
+e:0.2 m:1.0 e:0.3 m:1.1 hc:3 m:1.2 m:1.3 sa:0 n:1 qh:1 e:1.0 EQ:2 e:1.1 EQ:3
+e:1.2 m:2.0 e:1.3 m:2.1 EI:4 m:2.2 sa:1 m:2.3 n:2 ta:1.0 e:2.0 e:2.1 ta:0.0 e:2.2
+ta:1.1 ra:1.0 m:3.0 e:2.3 ta:0.1 ra:0.0 EQ:5 ra:1.1 EQ:4 m:3.1 EI:7 m:3.2 m:3.3 sb:1
+n:3 tb:1.0 ra:0.1 EQ:7 e:3.0 sb:0 sa:2 tb:1.1 e:3.1 rb:1.0 ta:2.0 rb:1.1 ta:2.1 e:3.2
+tb:0.0 e:3.3 ra:2.0 sc:1 tb:0.1 ra:2.1 tc:1.0 rb:0.0 sb:2 sa:3 tb:2.0 rb:0.1 tc:1.1 EI:6
+ta:3.0 sc:0 ta:3.1 cc:1.0 ra:3.0 tc:0.0 ra:3.1 EQ:6 tc:0.1 rb:2.0 sb:3 tb:2.1 cc:0.0 cc:0.1
+qc:0.0 qc:1.0 cc:1.1 qc:0.1 tb:3.0 rb:2.1 tb:3.1 rb:3.0 sc:2 oc:0.0 qc:1.1 tc:2.0 oc:0.1 rb:3.1
+tc:2.1 sc:3 oc:1.1 tc:3.0 cc:2.0 oc:1.0 tc:3.1 cc:2.1 cc:3.0 qc:2.0 qc:2.1 qc:3.0 cc:3.1 qc:3.1
+oc:2.0 oc:2.1 oc:3.0 oc:3.1
+""".split()
+ON_VECTOR = "W:0 W:2 W:6 EI:5 EI:3 oc:2.0 oc:3.0".split()
+
+
+def tile_specinferrecursiveresidualverify_kernel(tc, h_t, w_bytes, w_scale, q1, q2, g, emb, out):
+    nc = tc.nc
+    with ExitStack() as ctx:
+        keep = ctx.enter_context(tc.tile_pool(name="keep", bufs=1))
+        stage = ctx.enter_context(tc.tile_pool(name="stage", bufs=3))
+        psum = ctx.enter_context(tc.psum_pool(name="psum", bufs=1))
+
+        scale = keep.tile([P, 2, PACK], F32, name="scale")
+        w_view = w_bytes.rearrange("(g p t) n -> g p t n", p=P, t=PACK)
+        wb = {}
+        h_sb = []
+        emb_sb = {}
+        q_sb = {}
+        g_sb = keep.tile([P, V], BF16, name="g_sb")
+
+        def load_w(gg, c0, c1):
+            t = keep.tile([P, PACK, c1 - c0], U8, name=f"wb_{gg}_{c0}", align_bytes=64)
+            nc.sync.dma_start(out=t[:], in_=w_view[gg][:, :, c0:c1])
+            for c in range(c0, c1, CH):
+                wb[gg, c // CH] = t[:, :, c - c0 : c - c0 + CH]
+
+        def load_h(i):
+            t = keep.tile([P, D], BF16, name=f"h_{i}", align_bytes=64)
+            nc.sync.dma_start(out=t[:], in_=h_t[i * P : (i + 1) * P, :])
+            h_sb.append(t)
+
+        def load_q(i, which):
+            t = keep.tile([P, V], BF16, name=f"q{which}_{i}", align_bytes=64)
+            nc.sync.dma_start(out=t[:], in_=(q1, q2)[which - 1][i * P : (i + 1) * P, :])
+            q_sb[which, i] = t
+
+        def load_emb(k):
+            t = keep.tile([P, PACK, E], BF16, name=f"emb_{k}", align_bytes=64)
+            nc.sync.dma_start(out=t[:], in_=emb.rearrange("(g p t) n -> g p t n", p=P, t=PACK)[k])
+            emb_sb[k] = t
+
+        warm = keep.tile([P, 1], F32, name="warm")
+        nc.vector.memset(warm[:], 0.0)
+        nc.scalar.activation(out=warm[:], in_=warm[:], func=ACT.Exp)
+        ident = keep.tile([P, P], F32, name="ident")
+        make_identity(nc, ident[:])
+
+        nc.sync.dma_start(out=scale[:], in_=w_scale.rearrange("(g p t) o -> p g (t o)", p=P, t=PACK))
+        load_w(0, 0, 512)
+        load_w(1, 0, 512)
+        load_w(0, 512, 1024)
+        load_w(1, 512, 1024)
+        load_h(0)
+        load_h(1)
+        load_w(0, 1024, 2048)
+        load_w(1, 1024, 2048)
+        load_h(2)
+        load_h(3)
+        load_emb(0)
+        load_q(0, 1)
+        load_emb(1)
+        load_q(0, 2)
+        nc.sync.dma_start(out=g_sb[:], in_=g.partition_broadcast(P))
+        load_q(1, 1)
+        load_q(1, 2)
+        load_emb(2)
+        load_emb(3)
+        for i in (2, 3):
+            load_q(i, 1)
+            load_q(i, 2)
+
+        planes, grouped, w_codes, w_planes = {}, {}, {}, {}
+        h_group, h_codes = {}, {}
+        e_group, e_codes = {}, {}
+        c_group, c_codes = {}, {}
+        lt, work, stat, c_sb, acc = {}, {}, {}, {}, {}
+
+        def interleave(dst, src, engine):
+            o = dst.rearrange("p (c i) t -> p c t i", i=4)
+            s = src.rearrange("p t (c i) -> p c t i", i=4)
+            if engine == "V":
+                nc.vector.tensor_copy(out=o, in_=s)
+            else:
+                nc.scalar.copy(out=o, in_=s)
+
+        def widen(u, eng):
+            gg, j = u % 2, u // 2
+            t = stage.tile([P, PACK, CH], BF16, name="plane", align_bytes=64)
+            for k in range(PACK):
+                src = wb[gg, j][:, k, :].bitcast(F8)
+                s = scale[:, gg, k : k + 1]
+                if eng == "V":
+                    nc.vector.tensor_scalar(out=t[:, k, :], in0=src, scalar1=s, scalar2=None, op0=ALU.mult)
+                else:
+                    nc.scalar.activation(out=t[:, k, :], in_=src, func=ACT.Copy, scale=s)
+            planes[u] = t
+
+        def w_inter(u):
+            t = stage.tile([P, CH, PACK], BF16, name="grouped", tag="grouped", bufs=4, align_bytes=64)
+            interleave(t[:], planes[u][:], "V")
+            grouped[u] = t
+
+        def quant(codes, planes_, src):
+            nc.vector.quantize_mx(out=codes.bitcast(F8X4), scales=planes_, in_=src)
+
+        def w_quant(u):
+            cd = keep.tile([P, CH], U32, name=f"wc_{u}", align_bytes=64)
+            sc = keep.tile([P, CH], U8, name=f"ws_{u}", align_bytes=64)
+            quant(cd[:], sc[:], grouped[u][:].rearrange("p n t -> p (n t)"))
+            w_codes[u] = (cd, sc)
+
+        def h_turn(i):
+            words = h_sb[i][:].bitcast(F32)
+            tp = psum.tile([P, 2, 2, P], F32, name="tp", tag="tp", bufs=2)
+            for gg in range(2):
+                for k in range(2):
+                    nc.tensor.transpose(tp[:, gg, k, :], words[:, 256 * gg + k : 256 * (gg + 1) : 2], ident[:])
+            if i % 2 == 0:
+                h_group[i // 2] = stage.tile([P, 2, 2 * P, PACK], BF16, name="hg", tag="grouped", bufs=4, align_bytes=64)
+            dst = h_group[i // 2][:, i % 2, :, :].rearrange("p r t -> p (r t)").bitcast(F32)
+            nc.scalar.copy(
+                out=dst.rearrange("p (g r u) -> p g r u", g=2, u=2), in_=tp[:].rearrange("p g u r -> p g r u")
+            )
+
+        def h_quant(b):
+            cd = keep.tile([P, 2, 2, P], U32, name=f"hc_{b}", align_bytes=64)
+            sc = keep.tile([P, 2, 2, P], U8, name=f"hs_{b}", align_bytes=64)
+            quant(
+                cd[:].rearrange("p a g r -> p (a g r)"),
+                sc[:].rearrange("p a g r -> p (a g r)"),
+                h_group[b][:].rearrange("p a r t -> p (a r t)"),
+            )
+            for a in range(2):
+                h_codes[2 * b + a] = (cd[:, a], sc[:, a])
+
+        def e_inter(x, eng):
+            k, hf = x // 2, x % 2
+            t = stage.tile([P, CH, PACK], BF16, name="eg", align_bytes=64)
+            for z in range(2):
+                c0 = hf * CH + z * 256
+                interleave(t[:, z * 256 : (z + 1) * 256, :], emb_sb[k][:, :, c0 : c0 + 256], eng)
+            e_group[x] = t
+
+        def e_quant(x):
+            cd = keep.tile([P, CH], U32, name=f"ec_{x}", align_bytes=64)
+            sc = keep.tile([P, CH], U8, name=f"es_{x}", align_bytes=64)
+            quant(cd[:], sc[:], e_group[x][:].rearrange("p n t -> p (n t)"))
+            e_codes[x] = (cd, sc)
+
+        def mm1(i, j):
+            b = psum.tile([P, CH], F32, name=f"lt{j}", tag=f"lt{j}")
+            hc, hs = h_codes[i]
+            for gg in range(2):
+                wc, ws = w_codes[2 * j + gg]
+                nc.tensor.matmul_mx(
+                    out=b[:], lhsT=hc[:, gg, :].bitcast(F8X4), lhsT_scale=hs[:, gg, :],
+                    rhs=wc[:].bitcast(F8X4), rhs_scale=ws[:], start=gg == 0, stop=gg == 1,
+                )
+            lt[i, j] = b
+
+        def stats(i):
+            if i not in stat:
+                stat[i] = keep.tile([P, 32], F32, name=f"stat_{i}")
+                work[i] = keep.tile([P, V], F32, name=f"work_{i}", align_bytes=64)
+            return stat[i]
+
+        def rowmax(i, j):
+            mm1(i, j)
+            nc.vector.tensor_reduce(out=stats(i)[:, j : j + 1], in_=lt[i, j][:], axis=AX.X, op=ALU.max)
+
+        def negmax(i):
+            s = stats(i)
+            nc.vector.tensor_scalar(
+                out=s[:, 24:28], in0=s[:, 0:4], scalar1=-1.0, scalar2=None, op0=ALU.mult, op1=ALU.min, accum_out=s[:, 8:9]
+            )
+
+        def exp(i, j):
+            s = stats(i)
+            nc.scalar.activation(
+                out=work[i][:, j * CH : (j + 1) * CH], in_=lt[i, j][:], func=ACT.Exp, bias=s[:, 8:9], scale=1.0,
+                accum_out=s[:, 16 + j : 17 + j],
+            )
+
+        def mean(i, src, n, dst):
+            s = stats(i)
+            nc.vector.tensor_scalar(
+                out=s[:, 24 : 24 + n], in0=s[:, src : src + n], scalar1=INV_V, scalar2=None, op0=ALU.mult, op1=ALU.add,
+                accum_out=s[:, dst : dst + 1],
+            )
+
+        def resid(i, which, hf):
+            s = stats(i)
+            c = slice(hf * 1024, (hf + 1) * 1024)
+            nc.vector.scalar_tensor_tensor(
+                out=work[i][:, c], in0=q_sb[which, i][:, c], scalar=s[:, 8 + which : 9 + which], in1=work[i][:, c],
+                op0=ALU.mult, op1=ALU.subtract,
+            )
+
+        def relu(i, which, hf):
+            s = stats(i)
+            c = slice(hf * 1024, (hf + 1) * 1024)
+            col = 18 + 2 * which + hf
+            nc.scalar.activation(
+                out=work[i][:, c], in_=work[i][:, c], func=ACT.Relu, scale=-1.0, accum_out=s[:, col : col + 1]
+            )
+
+        def inv(i):
+            mean(i, 22, 2, 11)
+            s = stats(i)
+            nc.vector.reciprocal(out=s[:, 12:13], in_=s[:, 11:12])
+
+        def gain(i, hf):
+            s = stats(i)
+            if hf == 0:
+                c_sb[i] = stage.tile([P, V], BF16, name="c_sb", bufs=2, align_bytes=64)
+            c = slice(hf * 1024, (hf + 1) * 1024)
+            nc.vector.scalar_tensor_tensor(
+                out=c_sb[i][:, c], in0=work[i][:, c], scalar=s[:, 12:13], in1=g_sb[:, c], op0=ALU.mult, op1=ALU.mult
+            )
+
+        def c_turn(i, hf):
+            words = c_sb[i][:].bitcast(F32)
+            tp = psum.tile([P, 2, 2, P], F32, name="tp", tag="tp", bufs=2)
+            for gg in range(2):
+                w0 = 256 * (2 * hf + gg)
+                for k in range(2):
+                    nc.tensor.transpose(tp[:, gg, k, :], words[:, w0 + k : w0 + 256 : 2], ident[:])
+            t = stage.tile([P, 2 * P, PACK], BF16, name="cg", bufs=2, align_bytes=64)
+            nc.scalar.copy(
+                out=t[:].rearrange("p r t -> p (r t)").bitcast(F32).rearrange("p (g r u) -> p g r u", g=2, u=2),
+                in_=tp[:].rearrange("p g u r -> p g r u"),
+            )
+            c_group[i, hf] = t
+
+        def c_quant(i, hf):
+            cd = stage.tile([P, 2, P], U32, name="cc", bufs=4, align_bytes=64)
+            sc = stage.tile([P, 2, P], U8, name="cs", bufs=4, align_bytes=64)
+            quant(
+                cd[:].rearrange("p g r -> p (g r)"),
+                sc[:].rearrange("p g r -> p (g r)"),
+                c_group[i, hf][:].rearrange("p r t -> p (r t)"),
+            )
+            c_codes[i, hf] = (cd, sc)
+
+        def mm2(i, k):
+            if k == 0:
+                for hf in range(2):
+                    acc[i, hf] = psum.tile([P, CH], F32, name=f"acc{hf}", tag=f"acc{hf}")
+            cd, sc = c_codes[i, k // 2]
+            for hf in range(2):
+                ec, es = e_codes[2 * k + hf]
+                nc.tensor.matmul_mx(
+                    out=acc[i, hf][:], lhsT=cd[:, k % 2, :].bitcast(F8X4), lhsT_scale=sc[:, k % 2, :],
+                    rhs=ec[:].bitcast(F8X4), rhs_scale=es[:], start=k == 0, stop=k == 3,
+                )
+
+        def store(i, hf, eng):
+            if (i, 0) not in acc:
+                for k in range(4):
+                    mm2(i, k)
+            t = stage.tile([P, CH], F32, name="res", bufs=3, align_bytes=64)
+            if eng == "V":
+                nc.vector.tensor_copy(out=t[:], in_=acc[i, hf][:])
+            else:
+                nc.scalar.copy(out=t[:], in_=acc[i, hf][:])
+            nc.sync.dma_start(out=out[i * P : (i + 1) * P, hf * CH : (hf + 1) * CH], in_=t[:])
+
+        def run(step):
+            kind, rest = step.split(":")
+            a = [int(x) for x in rest.split(".")]
+            eng = "V" if step in ON_VECTOR else "S"
+            if kind == "W":
+                widen(a[0], eng)
+            elif kind == "I":
+                w_inter(a[0])
+            elif kind == "Q":
+                w_quant(a[0])
+            elif kind == "hc":
+                h_turn(a[0])
+            elif kind == "qh":
+                h_quant(a[0])
+            elif kind == "EI":
+                e_inter(a[0], eng)
+            elif kind == "EQ":
+                e_quant(a[0])
+            elif kind == "m":
+                rowmax(a[0], a[1])
+            elif kind == "n":
+                negmax(a[0])
+            elif kind == "e":
+                exp(a[0], a[1])
+            elif kind == "sa":
+                mean(a[0], 16, 4, 9)
+            elif kind == "ta":
+                resid(a[0], 1, a[1])
+            elif kind == "ra":
+                relu(a[0], 1, a[1])
+            elif kind == "sb":
+                mean(a[0], 20, 2, 10)
+            elif kind == "tb":
+                resid(a[0], 2, a[1])
+            elif kind == "rb":
+                relu(a[0], 2, a[1])
+            elif kind == "sc":
+                inv(a[0])
+            elif kind == "tc":
+                gain(a[0], a[1])
+            elif kind == "cc":
+                c_turn(a[0], a[1])
+            elif kind == "qc":
+                c_quant(a[0], a[1])
+            elif kind == "oc":
+                store(a[0], a[1], eng)
+
+        with tc.manual_schedule():
+            for step in ORDER:
+                run(step)

@@ -17,52 +17,58 @@ N, D, V, E = 512, 1024, 2048, 1024
 P = 128
 PACK = 4
 FLOPS = 2 * N * D * V + 2 * N * V * E
-TILES = N // P
 CH = 512
 INV_V = 1.0 / V
 
+UNITS = [(0, 0, 512), (1, 0, 512), (0, 512, 1024), (1, 512, 1024), (0, 1024, 2048), (1, 1024, 2048)]
+
 ORDER = """
-W:0 I:0 W:2 W:3 I:2 Q:0 W:1 W:6 I:3 hc:0 I:1 hc:1 W:4 Q:1
-I:6 W:5 Q:6 I:4 qh:0 EI:1 I:5 Q:4 Q:3 W:7 m:0.0 Q:5 EQ:1 Q:2
-EI:0 I:7 Q:7 m:0.1 hc:2 m:0.2 EI:2 m:0.3 EI:5 n:0 EQ:0 e:0.0 EI:3 e:0.1
-e:0.2 m:1.0 e:0.3 m:1.1 hc:3 m:1.2 m:1.3 sa:0 n:1 qh:1 e:1.0 EQ:2 e:1.1 EQ:3
-e:1.2 m:2.0 e:1.3 m:2.1 EI:4 m:2.2 sa:1 m:2.3 n:2 ta:1.0 e:2.0 e:2.1 ta:0.0 e:2.2
-ta:1.1 ra:1.0 m:3.0 e:2.3 ta:0.1 ra:0.0 EQ:5 ra:1.1 EQ:4 m:3.1 EI:7 m:3.2 m:3.3 sb:1
-n:3 tb:1.0 ra:0.1 EQ:7 e:3.0 sb:0 sa:2 tb:1.1 e:3.1 rb:1.0 ta:2.0 rb:1.1 ta:2.1 e:3.2
-tb:0.0 e:3.3 ra:2.0 sc:1 tb:0.1 ra:2.1 tc:1.0 rb:0.0 sb:2 sa:3 tb:2.0 rb:0.1 tc:1.1 EI:6
-ta:3.0 sc:0 ta:3.1 cc:1.0 ra:3.0 tc:0.0 ra:3.1 EQ:6 tc:0.1 rb:2.0 sb:3 tb:2.1 cc:0.0 cc:0.1
-qc:0.0 qc:1.0 cc:1.1 qc:0.1 tb:3.0 rb:2.1 tb:3.1 rb:3.0 sc:2 oc:0.0 qc:1.1 tc:2.0 oc:0.1 rb:3.1
-tc:2.1 sc:3 oc:1.1 tc:3.0 cc:2.0 oc:1.0 tc:3.1 cc:2.1 cc:3.0 qc:2.0 qc:2.1 qc:3.0 cc:3.1 qc:3.1
-oc:2.0 oc:2.1 oc:3.0 oc:3.1
+W:0 W:1 ht:0 I:1 hc:0 W:2 I:0 ht:1 Q:1 W:4 W:3 I:2 Q:0 ht:2
+Q:2 I:3 hc:1 I:4 EP:0 W:5 ht:3 qh:0 Q:4 mm:0.0 Q:3 EI:0 I:5 mm:0.1
+EP:1 EI:1 Q:5 hc:2 EP:2 m:0.0 m:0.1 mm:0.2 EI:2 mm:0.3 m:0.2 m:0.3 hc:3 EP:3
+n:0 qh:1 e:0.0 EQ:0 e:0.1 mm:1.0 e:0.2 mm:1.1 m:1.0 e:0.3 mm:1.2 m:1.1 EI:6 mm:1.3
+m:1.2 m:1.3 sa:0 n:1 ta:0 e:1.0 e:1.1 mm:2.0 e:1.2 mm:2.1 m:2.0 e:1.3 mm:2.2 m:2.1
+ra:0 mm:2.3 m:2.2 m:2.3 sa:1 n:2 e:2.0 sb:0 gs:0 EI:3 mm:3.0 ta:1 e:2.1 EP:4
+e:2.2 mm:3.1 e:2.3 EQ:1 mm:3.2 ra:1 mm:3.3 tb:0 EI:7 sa:2 m:3.0 sb:1 m:3.1 m:3.2
+rb:0 m:3.3 ta:2 EI:4 n:3 sc:0 EQ:3 e:3.0 EP:5 e:3.1 tb:1 e:3.2 e:3.3 EI:5
+sa:3 tc:0.0 ra:2 ta:3 rb:1 ct:0.0 ct:0.1 sb:2 EQ:2 cc:0.0 ra:3 sc:1 tb:2 cc:0.1
+sb:3 qc:0.0 rb:2 tb:3 o:0.0 o:0.1 sc:2 tc:1.0 rb:3 tc:2.0 oc:0.0 ct:1.0 ct:1.1 cc:1.0
+cc:1.1 sc:3 qc:1.0 ct:2.0 ct:2.1 oc:0.1 cc:2.0 o:1.0 tc:3.0 cc:2.1 o:1.1 oc:1.0 qc:2.0 ct:3.0
+oc:1.1 o:2.0 cc:3.0 tc:3.1 o:2.1 oc:2.0 qc:3.0 ct:3.1 oc:2.1 cc:3.1 oA:3 qc:3.1 o:3.0 o:3.1
+oc:3.0 oc:3.1
 """.split()
-ON_VECTOR = "W:0 W:2 W:6 EI:5 EI:3 oc:2.0 oc:3.0".split()
+ON_VECTOR = "W:1 W:3 oc:0.1 oc:1.0 oc:1.1".split()
+SPLIT = 3
 
 
 def tile_specinferrecursiveresidualverify_kernel(tc, h_t, w_bytes, w_scale, q1, q2, g, emb, out):
     nc = tc.nc
     with ExitStack() as ctx:
         keep = ctx.enter_context(tc.tile_pool(name="keep", bufs=1))
-        stage = ctx.enter_context(tc.tile_pool(name="stage", bufs=3))
+        stage = ctx.enter_context(tc.tile_pool(name="stage", bufs=2))
         psum = ctx.enter_context(tc.psum_pool(name="psum", bufs=1))
+
+        warm = keep.tile([P, 1], F32, name="warm")
+        nc.vector.memset(warm[:], 0.0)
+        nc.scalar.activation(out=warm[:], in_=warm[:], func=ACT.Exp)
+        ident = keep.tile([P, P], F32, name="ident")
+        make_identity(nc, ident[:])
+        ident16 = keep.tile([P, P], BF16, name="ident16")
+        make_identity(nc, ident16[:])
 
         scale = keep.tile([P, 2, PACK], F32, name="scale")
         w_view = w_bytes.rearrange("(g p t) n -> g p t n", p=P, t=PACK)
-        wb = {}
-        h_sb = []
-        emb_sb = {}
-        q_sb = {}
+        wb, h_sb, emb_sb, q_sb = {}, {}, {}, {}
         g_sb = keep.tile([P, V], BF16, name="g_sb")
 
-        def load_w(gg, c0, c1):
-            t = keep.tile([P, PACK, c1 - c0], U8, name=f"wb_{gg}_{c0}", align_bytes=64)
-            nc.sync.dma_start(out=t[:], in_=w_view[gg][:, :, c0:c1])
-            for c in range(c0, c1, CH):
-                wb[gg, c // CH] = t[:, :, c - c0 : c - c0 + CH]
+        def load_w(u):
+            gg, c0, c1 = UNITS[u]
+            wb[u] = keep.tile([P, PACK, c1 - c0], U8, name=f"wb_{u}", align_bytes=64)
+            nc.sync.dma_start(out=wb[u][:], in_=w_view[gg][:, :, c0:c1])
 
         def load_h(i):
-            t = keep.tile([P, D], BF16, name=f"h_{i}", align_bytes=64)
-            nc.sync.dma_start(out=t[:], in_=h_t[i * P : (i + 1) * P, :])
-            h_sb.append(t)
+            h_sb[i] = keep.tile([P, D], BF16, name=f"h_{i}", align_bytes=64)
+            nc.sync.dma_start(out=h_sb[i][:], in_=h_t[i * P : (i + 1) * P, :])
 
         def load_q(i, which):
             t = keep.tile([P, V], BF16, name=f"q{which}_{i}", align_bytes=64)
@@ -70,25 +76,18 @@ def tile_specinferrecursiveresidualverify_kernel(tc, h_t, w_bytes, w_scale, q1, 
             q_sb[which, i] = t
 
         def load_emb(k):
-            t = keep.tile([P, PACK, E], BF16, name=f"emb_{k}", align_bytes=64)
-            nc.sync.dma_start(out=t[:], in_=emb.rearrange("(g p t) n -> g p t n", p=P, t=PACK)[k])
-            emb_sb[k] = t
-
-        warm = keep.tile([P, 1], F32, name="warm")
-        nc.vector.memset(warm[:], 0.0)
-        nc.scalar.activation(out=warm[:], in_=warm[:], func=ACT.Exp)
-        ident = keep.tile([P, P], F32, name="ident")
-        make_identity(nc, ident[:])
+            emb_sb[k] = keep.tile([P, PACK, E], BF16, name=f"emb_{k}", align_bytes=64)
+            nc.sync.dma_start(out=emb_sb[k][:], in_=emb.rearrange("(g p t) n -> g p t n", p=P, t=PACK)[k])
 
         nc.sync.dma_start(out=scale[:], in_=w_scale.rearrange("(g p t) o -> p g (t o)", p=P, t=PACK))
-        load_w(0, 0, 512)
-        load_w(1, 0, 512)
-        load_w(0, 512, 1024)
-        load_w(1, 512, 1024)
+        load_w(0)
+        load_w(1)
         load_h(0)
+        load_w(2)
+        load_w(3)
         load_h(1)
-        load_w(0, 1024, 2048)
-        load_w(1, 1024, 2048)
+        load_w(4)
+        load_w(5)
         load_h(2)
         load_h(3)
         load_emb(0)
@@ -104,25 +103,29 @@ def tile_specinferrecursiveresidualverify_kernel(tc, h_t, w_bytes, w_scale, q1, 
             load_q(i, 1)
             load_q(i, 2)
 
-        planes, grouped, w_codes, w_planes = {}, {}, {}, {}
-        h_group, h_codes = {}, {}
-        e_group, e_codes = {}, {}
+        planes, grouped, w_codes = {}, {}, {}
+        tp, h_group, h_codes = {}, {}, {}
+        e_bank, e_group, e_codes = {}, {}, {}
         c_group, c_codes = {}, {}
         lt, work, stat, c_sb, acc = {}, {}, {}, {}, {}
 
-        def interleave(dst, src, engine):
-            o = dst.rearrange("p (c i) t -> p c t i", i=4)
-            s = src.rearrange("p t (c i) -> p c t i", i=4)
-            if engine == "V":
-                nc.vector.tensor_copy(out=o, in_=s)
+        def quant(codes, scales, src):
+            nc.vector.quantize_mx(out=codes.bitcast(F8X4), scales=scales, in_=src)
+
+        def copy(eng, dst, src):
+            if eng == "V":
+                nc.vector.tensor_copy(out=dst, in_=src)
             else:
-                nc.scalar.copy(out=o, in_=s)
+                nc.scalar.copy(out=dst, in_=src)
+
+        def interleave(eng, dst, src):
+            copy(eng, dst.rearrange("p (c i) t -> p c t i", i=4), src.rearrange("p t (c i) -> p c t i", i=4))
 
         def widen(u, eng):
-            gg, j = u % 2, u // 2
-            t = stage.tile([P, PACK, CH], BF16, name="plane", align_bytes=64)
+            gg, c0, c1 = UNITS[u]
+            t = stage.tile([P, PACK, c1 - c0], BF16, name="plane", tag="big", bufs=6, align_bytes=64)
             for k in range(PACK):
-                src = wb[gg, j][:, k, :].bitcast(F8)
+                src = wb[u][:, k, :].bitcast(F8)
                 s = scale[:, gg, k : k + 1]
                 if eng == "V":
                     nc.vector.tensor_scalar(out=t[:, k, :], in0=src, scalar1=s, scalar2=None, op0=ALU.mult)
@@ -131,31 +134,37 @@ def tile_specinferrecursiveresidualverify_kernel(tc, h_t, w_bytes, w_scale, q1, 
             planes[u] = t
 
         def w_inter(u):
-            t = stage.tile([P, CH, PACK], BF16, name="grouped", tag="grouped", bufs=4, align_bytes=64)
-            interleave(t[:], planes[u][:], "V")
-            grouped[u] = t
-
-        def quant(codes, planes_, src):
-            nc.vector.quantize_mx(out=codes.bitcast(F8X4), scales=planes_, in_=src)
+            gg, c0, c1 = UNITS[u]
+            grouped[u] = stage.tile([P, c1 - c0, PACK], BF16, name="grouped", tag="big", bufs=6, align_bytes=64)
+            interleave("V", grouped[u][:], planes[u][:])
 
         def w_quant(u):
-            cd = keep.tile([P, CH], U32, name=f"wc_{u}", align_bytes=64)
-            sc = keep.tile([P, CH], U8, name=f"ws_{u}", align_bytes=64)
+            gg, c0, c1 = UNITS[u]
+            cd = keep.tile([P, c1 - c0], U32, name=f"wc_{u}", align_bytes=64)
+            sc = keep.tile([P, c1 - c0], U8, name=f"ws_{u}", align_bytes=64)
             quant(cd[:], sc[:], grouped[u][:].rearrange("p n t -> p (n t)"))
-            w_codes[u] = (cd, sc)
+            for c in range(c0, c1, CH):
+                w_codes[gg, c // CH] = (cd[:, c - c0 : c - c0 + CH], sc[:, c - c0 : c - c0 + CH])
 
-        def h_turn(i):
-            words = h_sb[i][:].bitcast(F32)
-            tp = psum.tile([P, 2, 2, P], F32, name="tp", tag="tp", bufs=2)
+        def turn(key, words, w0):
+            tp[key] = psum.tile([P, 2, 2, P], F32, name="tp", tag="tp", bufs=2)
             for gg in range(2):
                 for k in range(2):
-                    nc.tensor.transpose(tp[:, gg, k, :], words[:, 256 * gg + k : 256 * (gg + 1) : 2], ident[:])
-            if i % 2 == 0:
-                h_group[i // 2] = stage.tile([P, 2, 2 * P, PACK], BF16, name="hg", tag="grouped", bufs=4, align_bytes=64)
-            dst = h_group[i // 2][:, i % 2, :, :].rearrange("p r t -> p (r t)").bitcast(F32)
-            nc.scalar.copy(
-                out=dst.rearrange("p (g r u) -> p g r u", g=2, u=2), in_=tp[:].rearrange("p g u r -> p g r u")
+                    a = w0 + 256 * gg + k
+                    nc.tensor.transpose(tp[key][:, gg, k, :], words[:, a : w0 + 256 * (gg + 1) : 2], ident[:])
+
+        def unturn(key, dst):
+            copy(
+                "S",
+                dst.rearrange("p r t -> p (r t)").bitcast(F32).rearrange("p (g r u) -> p g r u", g=2, u=2),
+                tp[key][:].rearrange("p g u r -> p g r u"),
             )
+
+        def h_copy(i):
+            b = i // 2
+            if i % 2 == 0:
+                h_group[b] = stage.tile([P, 2, 2 * P, PACK], BF16, name="hg", align_bytes=64)
+            unturn(("h", i), h_group[b][:, i % 2, :, :])
 
         def h_quant(b):
             cd = keep.tile([P, 2, 2, P], U32, name=f"hc_{b}", align_bytes=64)
@@ -168,136 +177,134 @@ def tile_specinferrecursiveresidualverify_kernel(tc, h_t, w_bytes, w_scale, q1, 
             for a in range(2):
                 h_codes[2 * b + a] = (cd[:, a], sc[:, a])
 
+        def e_turn(x):
+            k, hf = x // 2, x % 2
+            e_bank[x] = []
+            for z in range(2):
+                b = psum.tile([P, 256, PACK], BF16, name=f"ebank{z}", tag=f"acc{z}")
+                for y in range(2):
+                    c0 = hf * CH + z * 256 + y * P
+                    nc.tensor.matmul(
+                        b[:, y * P : (y + 1) * P, :],
+                        lhsT=ident16[:],
+                        rhs=emb_sb[k][:, :, c0 : c0 + P].rearrange("p t n -> p n t"),
+                        start=True,
+                        stop=True,
+                    )
+                e_bank[x].append(b)
+
         def e_inter(x, eng):
             k, hf = x // 2, x % 2
-            t = stage.tile([P, CH, PACK], BF16, name="eg", align_bytes=64)
-            for z in range(2):
-                c0 = hf * CH + z * 256
-                interleave(t[:, z * 256 : (z + 1) * 256, :], emb_sb[k][:, :, c0 : c0 + 256], eng)
-            e_group[x] = t
+            if k not in e_group:
+                e_group[k] = stage.tile([P, 2, CH, PACK], BF16, name="eg", align_bytes=64)
+            if x in e_bank:
+                for z in range(2):
+                    copy(eng, e_group[k][:, hf, z * 256 : (z + 1) * 256, :], e_bank[x][z][:])
+            else:
+                interleave(eng, e_group[k][:, hf, :, :], emb_sb[k][:, :, hf * CH : (hf + 1) * CH])
 
-        def e_quant(x):
-            cd = keep.tile([P, CH], U32, name=f"ec_{x}", align_bytes=64)
-            sc = keep.tile([P, CH], U8, name=f"es_{x}", align_bytes=64)
-            quant(cd[:], sc[:], e_group[x][:].rearrange("p n t -> p (n t)"))
-            e_codes[x] = (cd, sc)
+        def e_quant(k):
+            cd = keep.tile([P, 2, CH], U32, name=f"ec_{k}", align_bytes=64)
+            sc = keep.tile([P, 2, CH], U8, name=f"es_{k}", align_bytes=64)
+            quant(
+                cd[:].rearrange("p h n -> p (h n)"),
+                sc[:].rearrange("p h n -> p (h n)"),
+                e_group[k][:].rearrange("p h n t -> p (h n t)"),
+            )
+            e_codes[k] = (cd, sc)
 
         def mm1(i, j):
-            b = psum.tile([P, CH], F32, name=f"lt{j}", tag=f"lt{j}")
+            lt[i, j] = psum.tile([P, CH], F32, name=f"lt{j}", tag=f"lt{j}")
             hc, hs = h_codes[i]
             for gg in range(2):
-                wc, ws = w_codes[2 * j + gg]
+                wc, ws = w_codes[gg, j]
                 nc.tensor.matmul_mx(
-                    out=b[:], lhsT=hc[:, gg, :].bitcast(F8X4), lhsT_scale=hs[:, gg, :],
-                    rhs=wc[:].bitcast(F8X4), rhs_scale=ws[:], start=gg == 0, stop=gg == 1,
+                    out=lt[i, j][:], lhsT=hc[:, gg, :].bitcast(F8X4), lhsT_scale=hs[:, gg, :],
+                    rhs=wc.bitcast(F8X4), rhs_scale=ws, start=gg == 0, stop=gg == 1,
                 )
-            lt[i, j] = b
 
-        def stats(i):
+        def col(i, a, b=None):
             if i not in stat:
                 stat[i] = keep.tile([P, 32], F32, name=f"stat_{i}")
-                work[i] = keep.tile([P, V], F32, name=f"work_{i}", align_bytes=64)
-            return stat[i]
+            return stat[i][:, a : (a + 1 if b is None else b)]
 
         def rowmax(i, j):
-            mm1(i, j)
-            nc.vector.tensor_reduce(out=stats(i)[:, j : j + 1], in_=lt[i, j][:], axis=AX.X, op=ALU.max)
+            nc.vector.tensor_reduce(out=col(i, j), in_=lt[i, j][:], axis=AX.X, op=ALU.max)
 
         def negmax(i):
-            s = stats(i)
-            nc.vector.tensor_scalar(
-                out=s[:, 24:28], in0=s[:, 0:4], scalar1=-1.0, scalar2=None, op0=ALU.mult, op1=ALU.min, accum_out=s[:, 8:9]
-            )
+            nc.vector.tensor_reduce(out=col(i, 8), in_=col(i, 0, 4), axis=AX.X, op=ALU.max, negate=True)
 
         def exp(i, j):
-            s = stats(i)
+            if j == 0:
+                work[i] = stage.tile([P, V], F32, name="work", tag="big", bufs=6, align_bytes=64)
             nc.scalar.activation(
-                out=work[i][:, j * CH : (j + 1) * CH], in_=lt[i, j][:], func=ACT.Exp, bias=s[:, 8:9], scale=1.0,
-                accum_out=s[:, 16 + j : 17 + j],
+                out=work[i][:, j * CH : (j + 1) * CH], in_=lt[i, j][:], func=ACT.Exp, bias=col(i, 8), scale=1.0,
+                accum_out=col(i, 16 + j),
             )
 
-        def mean(i, src, n, dst):
-            s = stats(i)
+        def mean_e(i):
             nc.vector.tensor_scalar(
-                out=s[:, 24 : 24 + n], in0=s[:, src : src + n], scalar1=INV_V, scalar2=None, op0=ALU.mult, op1=ALU.add,
-                accum_out=s[:, dst : dst + 1],
+                out=col(i, 24, 28), in0=col(i, 16, 20), scalar1=INV_V, scalar2=None, op0=ALU.mult, op1=ALU.add,
+                accum_out=col(i, 9),
             )
 
-        def resid(i, which, hf):
-            s = stats(i)
-            c = slice(hf * 1024, (hf + 1) * 1024)
+        def mean_r(i):
+            nc.vector.tensor_scalar(out=col(i, 10), in0=col(i, 20), scalar1=INV_V, scalar2=None, op0=ALU.mult)
+
+        def resid(i, which):
             nc.vector.scalar_tensor_tensor(
-                out=work[i][:, c], in0=q_sb[which, i][:, c], scalar=s[:, 8 + which : 9 + which], in1=work[i][:, c],
+                out=work[i][:], in0=q_sb[which, i][:], scalar=col(i, 8 + which), in1=work[i][:],
                 op0=ALU.mult, op1=ALU.subtract,
             )
 
-        def relu(i, which, hf):
-            s = stats(i)
-            c = slice(hf * 1024, (hf + 1) * 1024)
-            col = 18 + 2 * which + hf
+        def relu(i, which):
             nc.scalar.activation(
-                out=work[i][:, c], in_=work[i][:, c], func=ACT.Relu, scale=-1.0, accum_out=s[:, col : col + 1]
+                out=work[i][:], in_=work[i][:], func=ACT.Relu, scale=-1.0, accum_out=col(i, 19 + which)
             )
 
         def inv(i):
-            mean(i, 22, 2, 11)
-            s = stats(i)
-            nc.vector.reciprocal(out=s[:, 12:13], in_=s[:, 11:12])
+            nc.vector.reciprocal(out=col(i, 11), in_=col(i, 21))
+
+        def gain_scale():
+            nc.vector.tensor_scalar(out=g_sb[:], in0=g_sb[:], scalar1=float(V), scalar2=None, op0=ALU.mult)
 
         def gain(i, hf):
-            s = stats(i)
             if hf == 0:
-                c_sb[i] = stage.tile([P, V], BF16, name="c_sb", bufs=2, align_bytes=64)
-            c = slice(hf * 1024, (hf + 1) * 1024)
+                c_sb[i] = stage.tile([P, V], BF16, name="c_sb", align_bytes=64)
+                c_group[i] = stage.tile([P, 4 * P, PACK], BF16, name="cg", align_bytes=64)
+                c_codes[i] = (
+                    stage.tile([P, 4, P], U32, name="cc", align_bytes=64),
+                    stage.tile([P, 4, P], U8, name="cs", align_bytes=64),
+                )
+            c = slice(hf * 1024, (hf + 1) * 1024) if i == SPLIT else slice(0, V)
             nc.vector.scalar_tensor_tensor(
-                out=c_sb[i][:, c], in0=work[i][:, c], scalar=s[:, 12:13], in1=g_sb[:, c], op0=ALU.mult, op1=ALU.mult
+                out=c_sb[i][:, c], in0=work[i][:, c], scalar=col(i, 11), in1=g_sb[:, c], op0=ALU.mult, op1=ALU.mult
             )
-
-        def c_turn(i, hf):
-            words = c_sb[i][:].bitcast(F32)
-            tp = psum.tile([P, 2, 2, P], F32, name="tp", tag="tp", bufs=2)
-            for gg in range(2):
-                w0 = 256 * (2 * hf + gg)
-                for k in range(2):
-                    nc.tensor.transpose(tp[:, gg, k, :], words[:, w0 + k : w0 + 256 : 2], ident[:])
-            t = stage.tile([P, 2 * P, PACK], BF16, name="cg", bufs=2, align_bytes=64)
-            nc.scalar.copy(
-                out=t[:].rearrange("p r t -> p (r t)").bitcast(F32).rearrange("p (g r u) -> p g r u", g=2, u=2),
-                in_=tp[:].rearrange("p g u r -> p g r u"),
-            )
-            c_group[i, hf] = t
 
         def c_quant(i, hf):
-            cd = stage.tile([P, 2, P], U32, name="cc", bufs=4, align_bytes=64)
-            sc = stage.tile([P, 2, P], U8, name="cs", bufs=4, align_bytes=64)
+            cd, sc = c_codes[i]
+            ks = slice(2 * hf, 2 * hf + 2) if i == SPLIT else slice(0, 4)
+            rs = slice(ks.start * P, ks.stop * P)
             quant(
-                cd[:].rearrange("p g r -> p (g r)"),
-                sc[:].rearrange("p g r -> p (g r)"),
-                c_group[i, hf][:].rearrange("p r t -> p (r t)"),
+                cd[:, ks, :].rearrange("p g r -> p (g r)"),
+                sc[:, ks, :].rearrange("p g r -> p (g r)"),
+                c_group[i][:, rs, :].rearrange("p r t -> p (r t)"),
             )
-            c_codes[i, hf] = (cd, sc)
 
-        def mm2(i, k):
-            if k == 0:
-                for hf in range(2):
-                    acc[i, hf] = psum.tile([P, CH], F32, name=f"acc{hf}", tag=f"acc{hf}")
-            cd, sc = c_codes[i, k // 2]
-            for hf in range(2):
-                ec, es = e_codes[2 * k + hf]
+        def mm2(i, hf, ks):
+            if (i, hf) not in acc:
+                acc[i, hf] = psum.tile([P, CH], F32, name=f"acc{hf}", tag=f"acc{hf}")
+            cd, sc = c_codes[i]
+            for k in ks:
+                ec, es = e_codes[k]
                 nc.tensor.matmul_mx(
-                    out=acc[i, hf][:], lhsT=cd[:, k % 2, :].bitcast(F8X4), lhsT_scale=sc[:, k % 2, :],
-                    rhs=ec[:].bitcast(F8X4), rhs_scale=es[:], start=k == 0, stop=k == 3,
+                    out=acc[i, hf][:], lhsT=cd[:, k, :].bitcast(F8X4), lhsT_scale=sc[:, k, :],
+                    rhs=ec[:, hf, :].bitcast(F8X4), rhs_scale=es[:, hf, :], start=k == 0, stop=k == 3,
                 )
 
         def store(i, hf, eng):
-            if (i, 0) not in acc:
-                for k in range(4):
-                    mm2(i, k)
             t = stage.tile([P, CH], F32, name="res", bufs=3, align_bytes=64)
-            if eng == "V":
-                nc.vector.tensor_copy(out=t[:], in_=acc[i, hf][:])
-            else:
-                nc.scalar.copy(out=t[:], in_=acc[i, hf][:])
+            copy(eng, t[:], acc[i, hf][:])
             nc.sync.dma_start(out=out[i * P : (i + 1) * P, hf * CH : (hf + 1) * CH], in_=t[:])
 
         def run(step):
@@ -310,14 +317,22 @@ def tile_specinferrecursiveresidualverify_kernel(tc, h_t, w_bytes, w_scale, q1, 
                 w_inter(a[0])
             elif kind == "Q":
                 w_quant(a[0])
+            elif kind == "ht":
+                turn(("h", a[0]), h_sb[a[0]][:].bitcast(F32), 0)
             elif kind == "hc":
-                h_turn(a[0])
+                h_copy(a[0])
             elif kind == "qh":
                 h_quant(a[0])
+            elif kind == "EP":
+                e_turn(a[0])
             elif kind == "EI":
                 e_inter(a[0], eng)
             elif kind == "EQ":
                 e_quant(a[0])
+            elif kind == "gs":
+                gain_scale()
+            elif kind == "mm":
+                mm1(a[0], a[1])
             elif kind == "m":
                 rowmax(a[0], a[1])
             elif kind == "n":
@@ -325,25 +340,32 @@ def tile_specinferrecursiveresidualverify_kernel(tc, h_t, w_bytes, w_scale, q1, 
             elif kind == "e":
                 exp(a[0], a[1])
             elif kind == "sa":
-                mean(a[0], 16, 4, 9)
+                mean_e(a[0])
             elif kind == "ta":
-                resid(a[0], 1, a[1])
+                resid(a[0], 1)
             elif kind == "ra":
-                relu(a[0], 1, a[1])
+                relu(a[0], 1)
             elif kind == "sb":
-                mean(a[0], 20, 2, 10)
+                mean_r(a[0])
             elif kind == "tb":
-                resid(a[0], 2, a[1])
+                resid(a[0], 2)
             elif kind == "rb":
-                relu(a[0], 2, a[1])
+                relu(a[0], 2)
             elif kind == "sc":
                 inv(a[0])
             elif kind == "tc":
                 gain(a[0], a[1])
+            elif kind == "ct":
+                turn(("c", a[0], a[1]), c_sb[a[0]][:].bitcast(F32), 512 * a[1])
             elif kind == "cc":
-                c_turn(a[0], a[1])
+                unturn(("c", a[0], a[1]), c_group[a[0]][:, 256 * a[1] : 256 * (a[1] + 1), :])
             elif kind == "qc":
                 c_quant(a[0], a[1])
+            elif kind == "oA":
+                for hf in range(2):
+                    mm2(a[0], hf, (0, 1))
+            elif kind == "o":
+                mm2(a[0], a[1], (2, 3) if a[0] == SPLIT else range(4))
             elif kind == "oc":
                 store(a[0], a[1], eng)
 

@@ -23,22 +23,23 @@ INV_V = 1.0 / V
 UNITS = [(0, 0, 512), (1, 0, 512), (0, 512, 1024), (1, 512, 1024), (0, 1024, 2048), (1, 1024, 2048)]
 
 ORDER = """
-W:0 W:1 ht:0 I:1 hc:0 W:2 I:0 ht:1 Q:1 W:4 W:3 I:2 Q:0 ht:2
-Q:2 I:3 hc:1 I:4 EP:0 W:5 ht:3 qh:0 Q:4 mm:0.0 Q:3 EI:0 I:5 mm:0.1
-EP:1 EI:1 Q:5 hc:2 EP:2 m:0.0 m:0.1 mm:0.2 EI:2 mm:0.3 m:0.2 m:0.3 hc:3 EP:3
-n:0 qh:1 e:0.0 EQ:0 e:0.1 mm:1.0 e:0.2 mm:1.1 m:1.0 e:0.3 mm:1.2 m:1.1 EI:6 mm:1.3
-m:1.2 m:1.3 sa:0 n:1 ta:0 e:1.0 e:1.1 mm:2.0 e:1.2 mm:2.1 m:2.0 e:1.3 mm:2.2 m:2.1
-ra:0 mm:2.3 m:2.2 m:2.3 sa:1 n:2 e:2.0 sb:0 gs:0 EI:3 mm:3.0 ta:1 e:2.1 EP:4
-e:2.2 mm:3.1 e:2.3 EQ:1 mm:3.2 ra:1 mm:3.3 tb:0 EI:7 sa:2 m:3.0 sb:1 m:3.1 m:3.2
-rb:0 m:3.3 ta:2 EI:4 n:3 sc:0 EQ:3 e:3.0 EP:5 e:3.1 tb:1 e:3.2 e:3.3 EI:5
-sa:3 tc:0.0 ra:2 ta:3 rb:1 ct:0.0 ct:0.1 sb:2 EQ:2 cc:0.0 ra:3 sc:1 tb:2 cc:0.1
-sb:3 qc:0.0 rb:2 tb:3 o:0.0 o:0.1 sc:2 tc:1.0 rb:3 tc:2.0 oc:0.0 ct:1.0 ct:1.1 cc:1.0
-cc:1.1 sc:3 qc:1.0 ct:2.0 ct:2.1 oc:0.1 cc:2.0 o:1.0 tc:3.0 cc:2.1 o:1.1 oc:1.0 qc:2.0 ct:3.0
-oc:1.1 o:2.0 cc:3.0 tc:3.1 o:2.1 oc:2.0 qc:3.0 ct:3.1 oc:2.1 cc:3.1 oA:3 qc:3.1 o:3.0 o:3.1
-oc:3.0 oc:3.1
+W:0.0 W:0.1 W:1.0 W:1.1 I:0 ht:0 W:2.1 I:1 W:3.1 W:3.0 ht:1 Q:0 W:2.0 I:3
+hc:0 W:4.1 hc:1 W:4.0 qh:0 ht:2 I:2 ht:3 W:5.0 I:4 EP:0 W:5.1 Q:3 Q:2
+Q:1 mm:0.1 EI:0 I:5 mm:0.0 hc:2 EP:1 hc:3 EI:1 Q:4 EP:2 Q:5 EI:2 m:0.0
+mm:0.2 m:0.1 mm:0.3 m:0.2 EP:3 m:0.3 n:0 EQ:0 e:0.0 e:0.1 mm:1.0 qh:1 e:0.2 mm:1.1
+m:1.0 e:0.3 mm:1.2 m:1.1 EI:7 mm:1.3 sa:0 m:1.2 m:1.3 n:1 ta:0 e:1.0 e:1.1 mm:2.0
+e:1.2 mm:2.1 e:1.3 m:2.0 mm:2.2 EI:3 m:2.1 mm:2.3 gs:0 EI:6 m:2.2 EP:4 m:2.3 sa:1
+EQ:1 ra:0 n:2 ta:1 e:2.0 EQ:3 e:2.1 mm:3.0 sb:0 ra:1 mm:3.1 tb:0 e:2.2 m:3.0
+sb:1 e:2.3 m:3.1 mm:3.2 rb:0 tb:1 mm:3.3 m:3.2 sa:2 rb:1 sc:0 m:3.3 ta:2 EI:4
+n:3 sc:1 ra:2 EP:5 tc:0.0 EI:5 tc:1.0 ct:0.0 ct:0.1 sb:2 e:3.0 e:3.1 tb:2 ct:1.0
+e:3.2 ct:1.1 e:3.3 sa:3 cc:0.0 EQ:2 rb:2 ta:3 cc:0.1 cc:1.0 sc:2 qc:0.0 cc:1.1 tc:2.0
+o:0.0 ra:3 o:0.1 qc:1.0 ct:2.0 sb:3 oc:0.1 tb:3 ct:2.1 oc:0.0 cc:2.0 o:1.1 cc:2.1 rb:3
+o:1.0 qc:2.0 oc:1.1 oc:1.0 o:2.1 sc:3 o:2.0 tc:3.0 oc:2.1 tc:3.1 tc:3.2 ct:3.0 oc:2.0 ct:3.1
+tc:3.3 ct:3.2 cc:3.0 cc:3.1 qc:3.0 ct:3.3 cc:3.2 qc:3.1 oa:3.0 cc:3.3 qc:3.2 oa:3.1 qc:3.3 oa:3.2
+o:3.0 o:3.1 oc:3.0 oc:3.1
 """.split()
-ON_VECTOR = "W:1 W:3 oc:0.1 oc:1.0 oc:1.1".split()
-SPLIT = 3
+ON_VECTOR = "W:0.0 W:1.0 W:3.0 W:4.1 sa:0 sa:1 oc:1.1 oc:1.0 oc:3.0".split()
+PARTS = (1, 1, 1, 4)
 
 
 def tile_specinferrecursiveresidualverify_kernel(tc, h_t, w_bytes, w_scale, q1, q2, g, emb, out):
@@ -63,8 +64,12 @@ def tile_specinferrecursiveresidualverify_kernel(tc, h_t, w_bytes, w_scale, q1, 
 
         def load_w(u):
             gg, c0, c1 = UNITS[u]
-            wb[u] = keep.tile([P, PACK, c1 - c0], U8, name=f"wb_{u}", align_bytes=64)
-            nc.sync.dma_start(out=wb[u][:], in_=w_view[gg][:, :, c0:c1])
+            step = 2 if u < 2 else PACK
+            for k in range(0, PACK, step):
+                t = keep.tile([P, step, c1 - c0], U8, name=f"wb_{u}_{k}", align_bytes=64)
+                nc.sync.dma_start(out=t[:], in_=w_view[gg][:, k : k + step, c0:c1])
+                for j in range(step):
+                    wb[u, k + j] = t[:, j, :]
 
         def load_h(i):
             h_sb[i] = keep.tile([P, D], BF16, name=f"h_{i}", align_bytes=64)
@@ -121,17 +126,18 @@ def tile_specinferrecursiveresidualverify_kernel(tc, h_t, w_bytes, w_scale, q1, 
         def interleave(eng, dst, src):
             copy(eng, dst.rearrange("p (c i) t -> p c t i", i=4), src.rearrange("p t (c i) -> p c t i", i=4))
 
-        def widen(u, eng):
+        def widen(u, half, eng):
             gg, c0, c1 = UNITS[u]
-            t = stage.tile([P, PACK, c1 - c0], BF16, name="plane", tag="big", bufs=6, align_bytes=64)
-            for k in range(PACK):
-                src = wb[u][:, k, :].bitcast(F8)
+            if u not in planes:
+                planes[u] = stage.tile([P, PACK, c1 - c0], BF16, name="plane", tag="big", bufs=6, align_bytes=64)
+            t = planes[u]
+            for k in (2 * half, 2 * half + 1):
+                src = wb[u, k].bitcast(F8)
                 s = scale[:, gg, k : k + 1]
                 if eng == "V":
                     nc.vector.tensor_scalar(out=t[:, k, :], in0=src, scalar1=s, scalar2=None, op0=ALU.mult)
                 else:
                     nc.scalar.activation(out=t[:, k, :], in_=src, func=ACT.Copy, scale=s)
-            planes[u] = t
 
         def w_inter(u):
             gg, c0, c1 = UNITS[u]
@@ -146,17 +152,18 @@ def tile_specinferrecursiveresidualverify_kernel(tc, h_t, w_bytes, w_scale, q1, 
             for c in range(c0, c1, CH):
                 w_codes[gg, c // CH] = (cd[:, c - c0 : c - c0 + CH], sc[:, c - c0 : c - c0 + CH])
 
-        def turn(key, words, w0):
-            tp[key] = psum.tile([P, 2, 2, P], F32, name="tp", tag="tp", bufs=2)
-            for gg in range(2):
+        def turn(key, words, passes):
+            tp[key] = psum.tile([P, len(passes), 2, P], F32, name="tp", tag="tp", bufs=2)
+            for b, gg in enumerate(passes):
                 for k in range(2):
-                    a = w0 + 256 * gg + k
-                    nc.tensor.transpose(tp[key][:, gg, k, :], words[:, a : w0 + 256 * (gg + 1) : 2], ident[:])
+                    nc.tensor.transpose(
+                        tp[key][:, b, k, :], words[:, 256 * gg + k : 256 * (gg + 1) : 2], ident[:]
+                    )
 
         def unturn(key, dst):
             copy(
                 "S",
-                dst.rearrange("p r t -> p (r t)").bitcast(F32).rearrange("p (g r u) -> p g r u", g=2, u=2),
+                dst.rearrange("p r t -> p (r t)").bitcast(F32).rearrange("p (g r u) -> p g r u", r=P, u=2),
                 tp[key][:].rearrange("p g u r -> p g r u"),
             )
 
@@ -242,13 +249,21 @@ def tile_specinferrecursiveresidualverify_kernel(tc, h_t, w_bytes, w_scale, q1, 
                 accum_out=col(i, 16 + j),
             )
 
-        def mean_e(i):
+        def mean_e(i, eng):
+            if eng == "S":
+                nc.scalar.activation(
+                    out=col(i, 24, 28), in_=col(i, 16, 20), func=ACT.Copy, scale=INV_V, accum_out=col(i, 9)
+                )
+                return
             nc.vector.tensor_scalar(
                 out=col(i, 24, 28), in0=col(i, 16, 20), scalar1=INV_V, scalar2=None, op0=ALU.mult, op1=ALU.add,
                 accum_out=col(i, 9),
             )
 
-        def mean_r(i):
+        def mean_r(i, eng):
+            if eng == "S":
+                nc.scalar.activation(out=col(i, 10), in_=col(i, 20), func=ACT.Copy, scale=INV_V)
+                return
             nc.vector.tensor_scalar(out=col(i, 10), in0=col(i, 20), scalar1=INV_V, scalar2=None, op0=ALU.mult)
 
         def resid(i, which):
@@ -268,6 +283,10 @@ def tile_specinferrecursiveresidualverify_kernel(tc, h_t, w_bytes, w_scale, q1, 
         def gain_scale():
             nc.vector.tensor_scalar(out=g_sb[:], in0=g_sb[:], scalar1=float(V), scalar2=None, op0=ALU.mult)
 
+        def c_passes(i, z):
+            n = 4 // max(PARTS[i], 2)
+            return range(z * n, (z + 1) * n)
+
         def gain(i, hf):
             if hf == 0:
                 c_sb[i] = stage.tile([P, V], BF16, name="c_sb", align_bytes=64)
@@ -276,15 +295,17 @@ def tile_specinferrecursiveresidualverify_kernel(tc, h_t, w_bytes, w_scale, q1, 
                     stage.tile([P, 4, P], U32, name="cc", align_bytes=64),
                     stage.tile([P, 4, P], U8, name="cs", align_bytes=64),
                 )
-            c = slice(hf * 1024, (hf + 1) * 1024) if i == SPLIT else slice(0, V)
+            n = V // PARTS[i]
+            c = slice(hf * n, (hf + 1) * n)
             nc.vector.scalar_tensor_tensor(
                 out=c_sb[i][:, c], in0=work[i][:, c], scalar=col(i, 11), in1=g_sb[:, c], op0=ALU.mult, op1=ALU.mult
             )
 
         def c_quant(i, hf):
             cd, sc = c_codes[i]
-            ks = slice(2 * hf, 2 * hf + 2) if i == SPLIT else slice(0, 4)
-            rs = slice(ks.start * P, ks.stop * P)
+            n = 4 // PARTS[i]
+            ks = slice(hf * n, (hf + 1) * n)
+            rs = slice(hf * n * P, (hf + 1) * n * P)
             quant(
                 cd[:, ks, :].rearrange("p g r -> p (g r)"),
                 sc[:, ks, :].rearrange("p g r -> p (g r)"),
@@ -312,13 +333,13 @@ def tile_specinferrecursiveresidualverify_kernel(tc, h_t, w_bytes, w_scale, q1, 
             a = [int(x) for x in rest.split(".")]
             eng = "V" if step in ON_VECTOR else "S"
             if kind == "W":
-                widen(a[0], eng)
+                widen(a[0], a[1], eng)
             elif kind == "I":
                 w_inter(a[0])
             elif kind == "Q":
                 w_quant(a[0])
             elif kind == "ht":
-                turn(("h", a[0]), h_sb[a[0]][:].bitcast(F32), 0)
+                turn(("h", a[0]), h_sb[a[0]][:].bitcast(F32), range(2))
             elif kind == "hc":
                 h_copy(a[0])
             elif kind == "qh":
@@ -340,13 +361,13 @@ def tile_specinferrecursiveresidualverify_kernel(tc, h_t, w_bytes, w_scale, q1, 
             elif kind == "e":
                 exp(a[0], a[1])
             elif kind == "sa":
-                mean_e(a[0])
+                mean_e(a[0], eng)
             elif kind == "ta":
                 resid(a[0], 1)
             elif kind == "ra":
                 relu(a[0], 1)
             elif kind == "sb":
-                mean_r(a[0])
+                mean_r(a[0], eng)
             elif kind == "tb":
                 resid(a[0], 2)
             elif kind == "rb":
@@ -356,16 +377,16 @@ def tile_specinferrecursiveresidualverify_kernel(tc, h_t, w_bytes, w_scale, q1, 
             elif kind == "tc":
                 gain(a[0], a[1])
             elif kind == "ct":
-                turn(("c", a[0], a[1]), c_sb[a[0]][:].bitcast(F32), 512 * a[1])
+                turn(("c", a[0], a[1]), c_sb[a[0]][:].bitcast(F32), c_passes(a[0], a[1]))
             elif kind == "cc":
-                unturn(("c", a[0], a[1]), c_group[a[0]][:, 256 * a[1] : 256 * (a[1] + 1), :])
+                unturn(("c", a[0], a[1]), c_group[a[0]][:, P * c_passes(a[0], a[1])[0] : P * (c_passes(a[0], a[1])[-1] + 1), :])
             elif kind == "qc":
                 c_quant(a[0], a[1])
-            elif kind == "oA":
+            elif kind == "oa":
                 for hf in range(2):
-                    mm2(a[0], hf, (0, 1))
+                    mm2(a[0], hf, (a[1],))
             elif kind == "o":
-                mm2(a[0], a[1], (2, 3) if a[0] == SPLIT else range(4))
+                mm2(a[0], a[1], range(PARTS[a[0]] - 1, 4))
             elif kind == "oc":
                 store(a[0], a[1], eng)
 

@@ -23,23 +23,24 @@ INV_V = 1.0 / V
 UNITS = [(0, 0, 512), (1, 0, 512), (0, 512, 1024), (1, 512, 1024), (0, 1024, 2048), (1, 1024, 2048)]
 
 ORDER = """
-W:0.0 W:0.1 W:1.0 W:1.1 I:0 ht:0 W:2.1 I:1 W:3.1 W:3.0 ht:1 Q:0 W:2.0 I:3
-hc:0 W:4.1 hc:1 W:4.0 qh:0 ht:2 I:2 ht:3 W:5.0 I:4 EP:0 W:5.1 Q:3 Q:2
-Q:1 mm:0.1 EI:0 I:5 mm:0.0 hc:2 EP:1 hc:3 EI:1 Q:4 EP:2 Q:5 EI:2 m:0.0
-mm:0.2 m:0.1 mm:0.3 m:0.2 EP:3 m:0.3 n:0 EQ:0 e:0.0 e:0.1 mm:1.0 qh:1 e:0.2 mm:1.1
-m:1.0 e:0.3 mm:1.2 m:1.1 EI:7 mm:1.3 sa:0 m:1.2 m:1.3 n:1 ta:0 e:1.0 e:1.1 mm:2.0
-e:1.2 mm:2.1 e:1.3 m:2.0 mm:2.2 EI:3 m:2.1 mm:2.3 gs:0 EI:6 m:2.2 EP:4 m:2.3 sa:1
-EQ:1 ra:0 n:2 ta:1 e:2.0 EQ:3 e:2.1 mm:3.0 sb:0 ra:1 mm:3.1 tb:0 e:2.2 m:3.0
-sb:1 e:2.3 m:3.1 mm:3.2 rb:0 tb:1 mm:3.3 m:3.2 sa:2 rb:1 sc:0 m:3.3 ta:2 EI:4
-n:3 sc:1 ra:2 EP:5 tc:0.0 EI:5 tc:1.0 ct:0.0 ct:0.1 sb:2 e:3.0 e:3.1 tb:2 ct:1.0
-e:3.2 ct:1.1 e:3.3 sa:3 cc:0.0 EQ:2 rb:2 ta:3 cc:0.1 cc:1.0 sc:2 qc:0.0 cc:1.1 tc:2.0
-o:0.0 ra:3 o:0.1 qc:1.0 ct:2.0 sb:3 oc:0.1 tb:3 ct:2.1 oc:0.0 cc:2.0 o:1.1 cc:2.1 rb:3
-o:1.0 qc:2.0 oc:1.1 oc:1.0 o:2.1 sc:3 o:2.0 tc:3.0 oc:2.1 tc:3.1 tc:3.2 ct:3.0 oc:2.0 ct:3.1
-tc:3.3 ct:3.2 cc:3.0 cc:3.1 qc:3.0 ct:3.3 cc:3.2 qc:3.1 oa:3.0 cc:3.3 qc:3.2 oa:3.1 qc:3.3 oa:3.2
+W:0.0 W:0.1 W:1.1 W:1.0 I:0 ht:0 W:2.1 W:2.0 I:1 hc:0 ht:1 W:3.1 I:2 W:3.0
+Q:1 hc:1 Q:0 W:5.1 I:3 ht:2 W:5.0 ht:3 hc:2 qh:0 W:4.1 I:5 mm:0.0 W:4.0
+Q:3 Q:5 EP:2 hc:3 I:4 EI:1 EP:3 Q:2 EI:2 Q:4 mm:0.1 EI:0 m:0.0 mm:0.2
+m:0.1 mm:0.3 m:0.2 m:0.3 EP:4 n:0 EQ:0 e:0.0 e:0.1 mm:1.0 gs:0 e:0.2 qh:1 mm:1.1
+e:0.3 m:1.0 mm:1.2 sa:0 m:1.1 EI:3 mm:1.3 m:1.2 EP:5 m:1.3 n:1 ta:0 e:1.0 e:1.1
+mm:2.0 e:1.2 mm:2.1 e:1.3 m:2.0 EI:4 mm:2.2 EQ:1 mm:2.3 EI:5 m:2.1 EP:6 m:2.2 sa:1
+ra:0 m:2.3 EQ:2 EP:7 n:2 ta:1 e:2.0 sb:0 e:2.1 mm:3.0 e:2.2 mm:3.1 tb:0 e:2.3
+mm:3.2 ra:1 mm:3.3 m:3.0 m:3.1 sa:2 sb:1 rb:0 m:3.2 tb:1 EI:6 m:3.3 rb:1 ta:2
+EI:7 sc:1 n:3 sc:0 tc:1.0 ra:2 tc:0.0 ct:1.0 e:3.0 ct:1.1 sb:2 e:3.1 cc:1.0 tb:2
+ct:0.0 e:3.2 e:3.3 ct:0.1 cc:0.0 EQ:3 cc:0.1 sa:3 cc:1.1 qc:0.0 rb:2 ta:3 o:0.0 o:0.1
+oc:0.0 sc:2 qc:1.0 ra:3 tc:2.0 o:1.0 sb:3 oc:0.1 tb:3 ct:2.0 oc:1.0 ct:2.1 cc:2.0 o:1.1
+cc:2.1 rb:3 qc:2.0 oc:1.1 o:2.0 sc:3 o:2.1 oc:2.0 tc:3.0 tc:3.1 tc:3.2 ct:3.0 oc:2.1 ct:3.1
+tc:3.3 cc:3.0 ct:3.2 cc:3.1 qc:3.0 ct:3.3 cc:3.2 qc:3.1 oa:3.0 cc:3.3 qc:3.2 qc:3.3 oa:3.1 oa:3.2
 o:3.0 o:3.1 oc:3.0 oc:3.1
 """.split()
-ON_VECTOR = "W:0.0 W:1.0 W:3.0 W:4.1 sa:0 sa:1 oc:1.1 oc:1.0 oc:3.0".split()
+ON_VECTOR = "W:0.0 W:1.1 I:0 W:2.0 I:1 I:2 I:3 W:5.0 I:5 I:4 oc:1.1 oc:3.1".split()
 PARTS = (1, 1, 1, 4)
+PAIRED = ()
 
 
 def tile_specinferrecursiveresidualverify_kernel(tc, h_t, w_bytes, w_scale, q1, q2, g, emb, out):
@@ -129,20 +130,28 @@ def tile_specinferrecursiveresidualverify_kernel(tc, h_t, w_bytes, w_scale, q1, 
         def widen(u, half, eng):
             gg, c0, c1 = UNITS[u]
             if u not in planes:
-                planes[u] = stage.tile([P, PACK, c1 - c0], BF16, name="plane", tag="big", bufs=6, align_bytes=64)
-            t = planes[u]
+                shape = [P, 2, c1 - c0, 2] if u in PAIRED else [P, PACK, c1 - c0]
+                planes[u] = stage.tile(shape, BF16, name="plane", tag="big", bufs=6, align_bytes=64)
             for k in (2 * half, 2 * half + 1):
                 src = wb[u, k].bitcast(F8)
                 s = scale[:, gg, k : k + 1]
+                dst = planes[u][:, k // 2, :, k % 2] if u in PAIRED else planes[u][:, k, :]
                 if eng == "V":
-                    nc.vector.tensor_scalar(out=t[:, k, :], in0=src, scalar1=s, scalar2=None, op0=ALU.mult)
+                    nc.vector.tensor_scalar(out=dst, in0=src, scalar1=s, scalar2=None, op0=ALU.mult)
                 else:
-                    nc.scalar.activation(out=t[:, k, :], in_=src, func=ACT.Copy, scale=s)
+                    nc.scalar.activation(out=dst, in_=src, func=ACT.Copy, scale=s)
 
-        def w_inter(u):
+        def w_inter(u, eng):
             gg, c0, c1 = UNITS[u]
             grouped[u] = stage.tile([P, c1 - c0, PACK], BF16, name="grouped", tag="big", bufs=6, align_bytes=64)
-            interleave("V", grouped[u][:], planes[u][:])
+            if u in PAIRED:
+                copy(
+                    eng,
+                    grouped[u][:].rearrange("p n t -> p (n t)").bitcast(F32).rearrange("p (n u) -> p n u", u=2),
+                    planes[u][:].rearrange("p u n e -> p (u n e)").bitcast(F32).rearrange("p (u n) -> p n u", u=2),
+                )
+            else:
+                interleave("V", grouped[u][:], planes[u][:])
 
         def w_quant(u):
             gg, c0, c1 = UNITS[u]
@@ -188,7 +197,10 @@ def tile_specinferrecursiveresidualverify_kernel(tc, h_t, w_bytes, w_scale, q1, 
             k, hf = x // 2, x % 2
             e_bank[x] = []
             for z in range(2):
-                b = psum.tile([P, 256, PACK], BF16, name=f"ebank{z}", tag=f"acc{z}")
+                if x % 2 == 0:
+                    b = psum.tile([P, 256, PACK], BF16, name=f"ebank{z}", tag=f"acc{z}")
+                else:
+                    b = psum.tile([P, 256, PACK], BF16, name=f"ebank{z}", tag="tp", bufs=2)
                 for y in range(2):
                     c0 = hf * CH + z * 256 + y * P
                     nc.tensor.matmul(
@@ -335,7 +347,7 @@ def tile_specinferrecursiveresidualverify_kernel(tc, h_t, w_bytes, w_scale, q1, 
             if kind == "W":
                 widen(a[0], a[1], eng)
             elif kind == "I":
-                w_inter(a[0])
+                w_inter(a[0], eng)
             elif kind == "Q":
                 w_quant(a[0])
             elif kind == "ht":

@@ -16,31 +16,56 @@ AX = mybir.AxisListType
 N, D, V, E = 512, 1024, 2048, 1024
 P = 128
 PACK = 4
-FLOPS = 2 * N * D * V + 2 * N * V * E
-CH = 512
+K_PASS = P * PACK
+BANK = 512
+D_PASSES = D // K_PASS
+V_PASSES = V // K_PASS
+CHUNKS = V // BANK
+HALVES = E // BANK
+PASS_WORDS = K_PASS // 2
+RUN = 4
+E_COLS = 256
+BIG_SLOTS = 6
 INV_V = 1.0 / V
 
-UNITS = [(0, 0, 512), (1, 0, 512), (0, 512, 1024), (1, 512, 1024), (0, 1024, 2048), (1, 1024, 2048)]
+FLOPS = 2 * N * D * V + 2 * N * V * E
 
-ORDER = """
-W:0.0 W:0.1 W:1.1 W:1.0 I:0 ht:0 W:2.1 W:2.0 I:1 hc:0 ht:1 W:3.1 I:2 W:3.0
-Q:1 hc:1 Q:0 W:5.1 I:3 ht:2 W:5.0 ht:3 hc:2 qh:0 W:4.1 I:5 mm:0.0 W:4.0
-Q:3 Q:5 EP:2 hc:3 I:4 EI:1 EP:3 Q:2 EI:2 Q:4 mm:0.1 EI:0 m:0.0 mm:0.2
-m:0.1 mm:0.3 m:0.2 m:0.3 EP:4 n:0 EQ:0 e:0.0 e:0.1 mm:1.0 gs:0 e:0.2 qh:1 mm:1.1
-e:0.3 m:1.0 mm:1.2 sa:0 m:1.1 EI:3 mm:1.3 m:1.2 EP:5 m:1.3 n:1 ta:0 e:1.0 e:1.1
-mm:2.0 e:1.2 mm:2.1 e:1.3 m:2.0 EI:4 mm:2.2 EQ:1 mm:2.3 EI:5 m:2.1 EP:6 m:2.2 sa:1
-ra:0 m:2.3 EQ:2 EP:7 n:2 ta:1 e:2.0 sb:0 e:2.1 mm:3.0 e:2.2 mm:3.1 tb:0 e:2.3
-mm:3.2 ra:1 mm:3.3 m:3.0 m:3.1 sa:2 sb:1 rb:0 m:3.2 tb:1 EI:6 m:3.3 rb:1 ta:2
-EI:7 sc:1 n:3 sc:0 tc:1.0 ra:2 tc:0.0 ct:1.0 e:3.0 ct:1.1 sb:2 e:3.1 cc:1.0 tb:2
-ct:0.0 e:3.2 e:3.3 ct:0.1 cc:0.0 EQ:3 cc:0.1 sa:3 cc:1.1 qc:0.0 rb:2 ta:3 o:0.0 o:0.1
-oc:0.0 sc:2 qc:1.0 ra:3 tc:2.0 o:1.0 sb:3 oc:0.1 tb:3 ct:2.0 oc:1.0 ct:2.1 cc:2.0 o:1.1
-cc:2.1 rb:3 qc:2.0 oc:1.1 o:2.0 sc:3 o:2.1 oc:2.0 tc:3.0 tc:3.1 tc:3.2 ct:3.0 oc:2.1 ct:3.1
-tc:3.3 cc:3.0 ct:3.2 cc:3.1 qc:3.0 ct:3.3 cc:3.2 qc:3.1 oa:3.0 cc:3.3 qc:3.2 qc:3.3 oa:3.1 oa:3.2
-o:3.0 o:3.1 oc:3.0 oc:3.1
-""".split()
-ON_VECTOR = "W:0.0 W:1.1 I:0 W:2.0 I:1 I:2 I:3 W:5.0 I:5 I:4 oc:1.1 oc:3.1".split()
+UNITS = ((0, 0, 512), (1, 0, 512), (0, 512, 1024), (1, 512, 1024), (0, 1024, 2048), (1, 1024, 2048))
+EARLY_UNITS = 2
+
 PARTS = (1, 1, 1, 4)
-PAIRED = ()
+
+MAXIMA = slice(0, 4)
+NEG_MAX = slice(4, 5)
+SUMS_E = slice(5, 9)
+MEAN_E = slice(9, 10)
+SUM_D1 = slice(10, 11)
+MEAN_D1 = slice(11, 12)
+SUM_D2 = slice(12, 13)
+INV_D2 = slice(13, 14)
+SCRATCH = 4
+
+ORDER = (
+    "widenV:0.0 widenV:0.1 widenS:1.1 weave_w:0 turn_h:0 widenV:2.1 widenS:2.0 quant_w:0 lift_h:0 widenV:3.0",
+    "turn_h:1 widenS:1.0 weave_w:2 lift_h:1 weave_w:1 widenS:3.1 widenV:5.1 widenS:5.0 turn_h:2 weave_w:3",
+    "turn_h:3 quant_h:0 widenS:4.0 quant_w:1 quant_w:2 mm1:0.0 quant_w:3 widenS:4.1 weave_w:5 mm1:0.1",
+    "lift_h:2 tensor_e:2 weave_w:4 lift_h:3 bring_eS:1 tensor_e:3 quant_w:5 bring_eS:0 quant_w:4 max:0.0",
+    "mm1:0.2 max:0.1 mm1:0.3 max:0.2 max:0.3 negmax:0",
+    "scale_gain: exp:0.0 quant_h:1 exp:0.1 mm1:1.0 quant_e:0 exp:0.2 mm1:1.1 exp:0.3 mm1:1.2 max:1.0",
+    "bring_eS:2 max:1.1 mm1:1.3 max:1.2 tensor_e:4 max:1.3 mean_eV:0 negmax:1 sub1:0 exp:1.0 exp:1.1 exp:1.2",
+    "mm1:2.0 exp:1.3 mm1:2.1 max:2.0 bring_eS:3 mm1:2.2 mean_eV:1 max:2.1 mm1:2.3 sub1:1 relu1:0 tensor_e:5",
+    "max:2.2 bring_eS:4 max:2.3 quant_e:1 mean_dS:0 relu1:1 tensor_e:6 negmax:2 sub2:0 exp:2.0 mean_dS:1",
+    "exp:2.1 mm1:3.0 sub2:1 exp:2.2 mm1:3.1 exp:2.3 mm1:3.2 bring_eS:5 mm1:3.3 max:3.0 mean_eS:2 relu2:0",
+    "tensor_e:7 quant_e:2 max:3.1 sub1:2 relu2:1 max:3.2 relu1:2 invert:0 invert:1 max:3.3 apply_gain:0.0",
+    "bring_eS:6 negmax:3 apply_gain:1.0 bring_eS:7 exp:3.0 turn_c:0.0 mean_dS:2 exp:3.1 turn_c:0.1 sub2:2",
+    "exp:3.2 lift_c:0.0 exp:3.3 turn_c:1.0 quant_e:3 lift_c:0.1 lift_c:1.0 turn_c:1.1 quant_c:0.0 mean_eS:3",
+    "relu2:2 sub1:3 last_passes:0.0 last_passes:0.1 lift_c:1.1 invert:2 relu1:3 apply_gain:2.0 quant_c:1.0",
+    "mean_dS:3 turn_c:2.0 storeS:0.1 sub2:3 storeS:0.0 turn_c:2.1 lift_c:2.0 last_passes:1.1 lift_c:2.1",
+    "quant_c:2.0 relu2:3 last_passes:1.0 storeV:1.1 last_passes:2.1 storeV:1.0 invert:3 last_passes:2.0",
+    "apply_gain:3.0 storeS:2.1 apply_gain:3.1 turn_c:3.0 apply_gain:3.2 storeS:2.0 turn_c:3.1 apply_gain:3.3",
+    "lift_c:3.0 lift_c:3.1 turn_c:3.2 quant_c:3.0 quant_c:3.1 turn_c:3.3 lift_c:3.2 one_pass:3.0 lift_c:3.3",
+    "quant_c:3.2 one_pass:3.1 quant_c:3.3 one_pass:3.2 last_passes:3.0 last_passes:3.1 storeV:3.0 storeS:3.1",
+)
 
 
 def tile_specinferrecursiveresidualverify_kernel(tc, h_t, w_bytes, w_scale, q1, q2, g, emb, out):
@@ -58,34 +83,34 @@ def tile_specinferrecursiveresidualverify_kernel(tc, h_t, w_bytes, w_scale, q1, 
         ident16 = keep.tile([P, P], BF16, name="ident16")
         make_identity(nc, ident16[:])
 
-        scale = keep.tile([P, 2, PACK], F32, name="scale")
-        w_view = w_bytes.rearrange("(g p t) n -> g p t n", p=P, t=PACK)
-        wb, h_sb, emb_sb, q_sb = {}, {}, {}, {}
-        g_sb = keep.tile([P, V], BF16, name="g_sb")
+        w_factor = keep.tile([P, D_PASSES, PACK], F32, name="w_factor")
+        w_rows = w_bytes.rearrange("(g p t) n -> g p t n", p=P, t=PACK)
+        emb_rows = emb.rearrange("(g p t) n -> g p t n", p=P, t=PACK)
+        byte_plane, h_in, emb_in, q_in = {}, {}, {}, {}
+        gain = keep.tile([P, V], BF16, name="gain")
 
         def load_w(u):
-            gg, c0, c1 = UNITS[u]
-            step = 2 if u < 2 else PACK
-            for k in range(0, PACK, step):
-                t = keep.tile([P, step, c1 - c0], U8, name=f"wb_{u}_{k}", align_bytes=64)
-                nc.sync.dma_start(out=t[:], in_=w_view[gg][:, k : k + step, c0:c1])
-                for j in range(step):
-                    wb[u, k + j] = t[:, j, :]
+            k_pass, c0, c1 = UNITS[u]
+            planes = 2 if u < EARLY_UNITS else PACK
+            for t0 in range(0, PACK, planes):
+                w_byte = keep.tile([P, planes, c1 - c0], U8, name=f"w_byte_{u}_{t0}", align_bytes=64)
+                nc.sync.dma_start(out=w_byte[:], in_=w_rows[k_pass][:, t0 : t0 + planes, c0:c1])
+                for t in range(planes):
+                    byte_plane[u, t0 + t] = w_byte[:, t, :]
 
         def load_h(i):
-            h_sb[i] = keep.tile([P, D], BF16, name=f"h_{i}", align_bytes=64)
-            nc.sync.dma_start(out=h_sb[i][:], in_=h_t[i * P : (i + 1) * P, :])
+            h_in[i] = keep.tile([P, D], BF16, name=f"h_{i}", align_bytes=64)
+            nc.sync.dma_start(out=h_in[i][:], in_=h_t[i * P : (i + 1) * P, :])
 
         def load_q(i, which):
-            t = keep.tile([P, V], BF16, name=f"q{which}_{i}", align_bytes=64)
-            nc.sync.dma_start(out=t[:], in_=(q1, q2)[which - 1][i * P : (i + 1) * P, :])
-            q_sb[which, i] = t
+            q_in[which, i] = keep.tile([P, V], BF16, name=f"q{which}_{i}", align_bytes=64)
+            nc.sync.dma_start(out=q_in[which, i][:], in_=(q1, q2)[which - 1][i * P : (i + 1) * P, :])
 
-        def load_emb(k):
-            emb_sb[k] = keep.tile([P, PACK, E], BF16, name=f"emb_{k}", align_bytes=64)
-            nc.sync.dma_start(out=emb_sb[k][:], in_=emb.rearrange("(g p t) n -> g p t n", p=P, t=PACK)[k])
+        def load_emb(k_pass):
+            emb_in[k_pass] = keep.tile([P, PACK, E], BF16, name=f"emb_{k_pass}", align_bytes=64)
+            nc.sync.dma_start(out=emb_in[k_pass][:], in_=emb_rows[k_pass])
 
-        nc.sync.dma_start(out=scale[:], in_=w_scale.rearrange("(g p t) o -> p g (t o)", p=P, t=PACK))
+        nc.sync.dma_start(out=w_factor[:], in_=w_scale.rearrange("(g p t) o -> p g (t o)", p=P, t=PACK))
         load_w(0)
         load_w(1)
         load_h(0)
@@ -100,7 +125,7 @@ def tile_specinferrecursiveresidualverify_kernel(tc, h_t, w_bytes, w_scale, q1, 
         load_q(0, 1)
         load_emb(1)
         load_q(0, 2)
-        nc.sync.dma_start(out=g_sb[:], in_=g.partition_broadcast(P))
+        nc.sync.dma_start(out=gain[:], in_=g.partition_broadcast(P))
         load_q(1, 1)
         load_q(1, 2)
         load_emb(2)
@@ -109,299 +134,312 @@ def tile_specinferrecursiveresidualverify_kernel(tc, h_t, w_bytes, w_scale, q1, 
             load_q(i, 1)
             load_q(i, 2)
 
-        planes, grouped, w_codes = {}, {}, {}
-        tp, h_group, h_codes = {}, {}, {}
-        e_bank, e_group, e_codes = {}, {}, {}
-        c_group, c_codes = {}, {}
-        lt, work, stat, c_sb, acc = {}, {}, {}, {}, {}
-
-        def quant(codes, scales, src):
-            nc.vector.quantize_mx(out=codes.bitcast(F8X4), scales=scales, in_=src)
-
-        def copy(eng, dst, src):
-            if eng == "V":
+        def copy(engine, dst, src):
+            if engine == "V":
                 nc.vector.tensor_copy(out=dst, in_=src)
             else:
                 nc.scalar.copy(out=dst, in_=src)
 
-        def interleave(eng, dst, src):
-            copy(eng, dst.rearrange("p (c i) t -> p c t i", i=4), src.rearrange("p t (c i) -> p c t i", i=4))
+        def weave(engine, dst, src):
+            copy(engine, dst.rearrange("p (c i) t -> p c t i", i=RUN), src.rearrange("p t (c i) -> p c t i", i=RUN))
 
-        def widen(u, half, eng):
-            gg, c0, c1 = UNITS[u]
-            if u not in planes:
-                shape = [P, 2, c1 - c0, 2] if u in PAIRED else [P, PACK, c1 - c0]
-                planes[u] = stage.tile(shape, BF16, name="plane", tag="big", bufs=6, align_bytes=64)
-            for k in (2 * half, 2 * half + 1):
-                src = wb[u, k].bitcast(F8)
-                s = scale[:, gg, k : k + 1]
-                dst = planes[u][:, k // 2, :, k % 2] if u in PAIRED else planes[u][:, k, :]
-                if eng == "V":
-                    nc.vector.tensor_scalar(out=dst, in0=src, scalar1=s, scalar2=None, op0=ALU.mult)
-                else:
-                    nc.scalar.activation(out=dst, in_=src, func=ACT.Copy, scale=s)
+        def quantise(codes, scales, src):
+            nc.vector.quantize_mx(out=codes.bitcast(F8X4), scales=scales, in_=src)
 
-        def w_inter(u, eng):
-            gg, c0, c1 = UNITS[u]
-            grouped[u] = stage.tile([P, c1 - c0, PACK], BF16, name="grouped", tag="big", bufs=6, align_bytes=64)
-            if u in PAIRED:
-                copy(
-                    eng,
-                    grouped[u][:].rearrange("p n t -> p (n t)").bitcast(F32).rearrange("p (n u) -> p n u", u=2),
-                    planes[u][:].rearrange("p u n e -> p (u n e)").bitcast(F32).rearrange("p (u n) -> p n u", u=2),
-                )
-            else:
-                interleave("V", grouped[u][:], planes[u][:])
+        def big(shape, dtype, name):
+            return stage.tile(shape, dtype, name=name, tag="big", bufs=BIG_SLOTS, align_bytes=64)
 
-        def w_quant(u):
-            gg, c0, c1 = UNITS[u]
-            cd = keep.tile([P, c1 - c0], U32, name=f"wc_{u}", align_bytes=64)
-            sc = keep.tile([P, c1 - c0], U8, name=f"ws_{u}", align_bytes=64)
-            quant(cd[:], sc[:], grouped[u][:].rearrange("p n t -> p (n t)"))
-            for c in range(c0, c1, CH):
-                w_codes[gg, c // CH] = (cd[:, c - c0 : c - c0 + CH], sc[:, c - c0 : c - c0 + CH])
+        def turn(bank, words, passes):
+            for b, k_pass in enumerate(passes):
+                for u in range(2):
+                    every_second = slice(PASS_WORDS * k_pass + u, PASS_WORDS * (k_pass + 1), 2)
+                    nc.tensor.transpose(bank[:, b, u, :], words[:, every_second], ident[:])
 
-        def turn(key, words, passes):
-            tp[key] = psum.tile([P, len(passes), 2, P], F32, name="tp", tag="tp", bufs=2)
-            for b, gg in enumerate(passes):
-                for k in range(2):
-                    nc.tensor.transpose(
-                        tp[key][:, b, k, :], words[:, 256 * gg + k : 256 * (gg + 1) : 2], ident[:]
-                    )
-
-        def unturn(key, dst):
-            copy(
-                "S",
-                dst.rearrange("p r t -> p (r t)").bitcast(F32).rearrange("p (g r u) -> p g r u", r=P, u=2),
-                tp[key][:].rearrange("p g u r -> p g r u"),
+        def lift(dst, bank):
+            nc.scalar.copy(
+                out=dst.rearrange("p r t -> p (r t)").bitcast(F32).rearrange("p (g r u) -> p g r u", r=P, u=2),
+                in_=bank[:].rearrange("p g u r -> p g r u"),
             )
 
-        def h_copy(i):
-            b = i // 2
-            if i % 2 == 0:
-                h_group[b] = stage.tile([P, 2, 2 * P, PACK], BF16, name="hg", align_bytes=64)
-            unturn(("h", i), h_group[b][:, i % 2, :, :])
+        w_planes, w_woven, w_codes = {}, {}, {}
 
-        def h_quant(b):
-            cd = keep.tile([P, 2, 2, P], U32, name=f"hc_{b}", align_bytes=64)
-            sc = keep.tile([P, 2, 2, P], U8, name=f"hs_{b}", align_bytes=64)
-            quant(
-                cd[:].rearrange("p a g r -> p (a g r)"),
-                sc[:].rearrange("p a g r -> p (a g r)"),
-                h_group[b][:].rearrange("p a r t -> p (a r t)"),
+        def widen(engine, u, pair):
+            k_pass, c0, c1 = UNITS[u]
+            if u not in w_planes:
+                w_planes[u] = big([P, PACK, c1 - c0], BF16, "w_planes")
+            for t in (2 * pair, 2 * pair + 1):
+                src = byte_plane[u, t].bitcast(F8)
+                factor = w_factor[:, k_pass, t : t + 1]
+                if engine == "V":
+                    nc.vector.tensor_scalar(
+                        out=w_planes[u][:, t, :], in0=src, scalar1=factor, scalar2=None, op0=ALU.mult
+                    )
+                else:
+                    nc.scalar.activation(out=w_planes[u][:, t, :], in_=src, func=ACT.Copy, scale=factor)
+
+        def weave_w(u):
+            k_pass, c0, c1 = UNITS[u]
+            w_woven[u] = big([P, c1 - c0, PACK], BF16, "w_woven")
+            weave("V", w_woven[u][:], w_planes[u][:])
+
+        def quant_w(u):
+            k_pass, c0, c1 = UNITS[u]
+            codes = keep.tile([P, c1 - c0], U32, name=f"w_codes_{u}", align_bytes=64)
+            scales = keep.tile([P, c1 - c0], U8, name=f"w_scales_{u}", align_bytes=64)
+            quantise(codes[:], scales[:], w_woven[u][:].rearrange("p n t -> p (n t)"))
+            for c in range(c0, c1, BANK):
+                cols = slice(c - c0, c - c0 + BANK)
+                w_codes[k_pass, c // BANK] = (codes[:, cols], scales[:, cols])
+
+        h_bank, h_woven, h_codes = {}, {}, {}
+
+        def turn_h(i):
+            h_bank[i] = psum.tile([P, D_PASSES, 2, P], F32, name="turned", tag="turned", bufs=2)
+            turn(h_bank[i], h_in[i][:].bitcast(F32), range(D_PASSES))
+
+        def lift_h(i):
+            pair = i // 2
+            if i % 2 == 0:
+                h_woven[pair] = stage.tile([P, 2, D_PASSES * P, PACK], BF16, name="h_woven", align_bytes=64)
+            lift(h_woven[pair][:, i % 2, :, :], h_bank[i])
+
+        def quant_h(pair):
+            codes = keep.tile([P, 2, D_PASSES, P], U32, name=f"h_codes_{pair}", align_bytes=64)
+            scales = keep.tile([P, 2, D_PASSES, P], U8, name=f"h_scales_{pair}", align_bytes=64)
+            quantise(
+                codes[:].rearrange("p a g r -> p (a g r)"),
+                scales[:].rearrange("p a g r -> p (a g r)"),
+                h_woven[pair][:].rearrange("p a r t -> p (a r t)"),
             )
             for a in range(2):
-                h_codes[2 * b + a] = (cd[:, a], sc[:, a])
+                h_codes[2 * pair + a] = (codes[:, a], scales[:, a])
 
-        def e_turn(x):
-            k, hf = x // 2, x % 2
-            e_bank[x] = []
-            for z in range(2):
+        e_banks, e_woven, e_codes = {}, {}, {}
+
+        def weave_e_on_tensor(x):
+            k_pass, half = divmod(x, 2)
+            e_banks[x] = []
+            for z in range(BANK // E_COLS):
                 if x % 2 == 0:
-                    b = psum.tile([P, 256, PACK], BF16, name=f"ebank{z}", tag=f"acc{z}")
+                    bank = psum.tile([P, E_COLS, PACK], BF16, name=f"e_bank{z}", tag=f"acc{z}")
                 else:
-                    b = psum.tile([P, 256, PACK], BF16, name=f"ebank{z}", tag="tp", bufs=2)
-                for y in range(2):
-                    c0 = hf * CH + z * 256 + y * P
+                    bank = psum.tile([P, E_COLS, PACK], BF16, name=f"e_bank{z}", tag="turned", bufs=2)
+                for y in range(E_COLS // P):
+                    c0 = half * BANK + z * E_COLS + y * P
                     nc.tensor.matmul(
-                        b[:, y * P : (y + 1) * P, :],
+                        bank[:, y * P : (y + 1) * P, :].rearrange("p (c i) t -> p c t i", i=RUN),
                         lhsT=ident16[:],
-                        rhs=emb_sb[k][:, :, c0 : c0 + P].rearrange("p t n -> p n t"),
+                        rhs=emb_in[k_pass][:, :, c0 : c0 + P].rearrange("p t (c i) -> p c t i", i=RUN),
                         start=True,
                         stop=True,
                     )
-                e_bank[x].append(b)
+                e_banks[x].append(bank)
 
-        def e_inter(x, eng):
-            k, hf = x // 2, x % 2
-            if k not in e_group:
-                e_group[k] = stage.tile([P, 2, CH, PACK], BF16, name="eg", align_bytes=64)
-            if x in e_bank:
-                for z in range(2):
-                    copy(eng, e_group[k][:, hf, z * 256 : (z + 1) * 256, :], e_bank[x][z][:])
+        def bring_e(engine, x):
+            k_pass, half = divmod(x, 2)
+            if k_pass not in e_woven:
+                e_woven[k_pass] = stage.tile([P, HALVES, BANK, PACK], BF16, name="e_woven", align_bytes=64)
+            if x in e_banks:
+                for z in range(BANK // E_COLS):
+                    copy(engine, e_woven[k_pass][:, half, z * E_COLS : (z + 1) * E_COLS, :], e_banks[x][z][:])
             else:
-                interleave(eng, e_group[k][:, hf, :, :], emb_sb[k][:, :, hf * CH : (hf + 1) * CH])
+                weave(engine, e_woven[k_pass][:, half, :, :], emb_in[k_pass][:, :, half * BANK : (half + 1) * BANK])
 
-        def e_quant(k):
-            cd = keep.tile([P, 2, CH], U32, name=f"ec_{k}", align_bytes=64)
-            sc = keep.tile([P, 2, CH], U8, name=f"es_{k}", align_bytes=64)
-            quant(
-                cd[:].rearrange("p h n -> p (h n)"),
-                sc[:].rearrange("p h n -> p (h n)"),
-                e_group[k][:].rearrange("p h n t -> p (h n t)"),
+        def quant_e(k_pass):
+            codes = keep.tile([P, HALVES, BANK], U32, name=f"e_codes_{k_pass}", align_bytes=64)
+            scales = keep.tile([P, HALVES, BANK], U8, name=f"e_scales_{k_pass}", align_bytes=64)
+            quantise(
+                codes[:].rearrange("p h n -> p (h n)"),
+                scales[:].rearrange("p h n -> p (h n)"),
+                e_woven[k_pass][:].rearrange("p h n t -> p (h n t)"),
             )
-            e_codes[k] = (cd, sc)
+            e_codes[k_pass] = (codes, scales)
 
-        def mm1(i, j):
-            lt[i, j] = psum.tile([P, CH], F32, name=f"lt{j}", tag=f"lt{j}")
-            hc, hs = h_codes[i]
-            for gg in range(2):
-                wc, ws = w_codes[gg, j]
+        lt, rows, stats = {}, {}, {}
+
+        def stat(i, cols):
+            if i not in stats:
+                stats[i] = keep.tile([P, 32], F32, name=f"stats_{i}")
+            return stats[i][:, cols]
+
+        def first_matmul(i, j):
+            lt[i, j] = psum.tile([P, BANK], F32, name=f"lt{j}", tag=f"lt{j}")
+            h_c, h_s = h_codes[i]
+            for k_pass in range(D_PASSES):
+                w_c, w_s = w_codes[k_pass, j]
                 nc.tensor.matmul_mx(
-                    out=lt[i, j][:], lhsT=hc[:, gg, :].bitcast(F8X4), lhsT_scale=hs[:, gg, :],
-                    rhs=wc.bitcast(F8X4), rhs_scale=ws, start=gg == 0, stop=gg == 1,
+                    out=lt[i, j][:],
+                    lhsT=h_c[:, k_pass, :].bitcast(F8X4),
+                    lhsT_scale=h_s[:, k_pass, :],
+                    rhs=w_c.bitcast(F8X4),
+                    rhs_scale=w_s,
+                    start=k_pass == 0,
+                    stop=k_pass == D_PASSES - 1,
                 )
 
-        def col(i, a, b=None):
-            if i not in stat:
-                stat[i] = keep.tile([P, 32], F32, name=f"stat_{i}")
-            return stat[i][:, a : (a + 1 if b is None else b)]
+        def row_max(i, j):
+            nc.vector.tensor_reduce(out=stat(i, MAXIMA)[:, j : j + 1], in_=lt[i, j][:], axis=AX.X, op=ALU.max)
 
-        def rowmax(i, j):
-            nc.vector.tensor_reduce(out=col(i, j), in_=lt[i, j][:], axis=AX.X, op=ALU.max)
-
-        def negmax(i):
-            nc.vector.tensor_reduce(out=col(i, 8), in_=col(i, 0, 4), axis=AX.X, op=ALU.max, negate=True)
+        def neg_max(i):
+            nc.vector.tensor_reduce(
+                out=stat(i, NEG_MAX), in_=stat(i, MAXIMA), axis=AX.X, op=ALU.max, negate=True
+            )
 
         def exp(i, j):
             if j == 0:
-                work[i] = stage.tile([P, V], F32, name="work", tag="big", bufs=6, align_bytes=64)
+                rows[i] = big([P, V], F32, "rows")
             nc.scalar.activation(
-                out=work[i][:, j * CH : (j + 1) * CH], in_=lt[i, j][:], func=ACT.Exp, bias=col(i, 8), scale=1.0,
-                accum_out=col(i, 16 + j),
+                out=rows[i][:, j * BANK : (j + 1) * BANK],
+                in_=lt[i, j][:],
+                func=ACT.Exp,
+                bias=stat(i, NEG_MAX),
+                scale=1.0,
+                accum_out=stat(i, SUMS_E)[:, j : j + 1],
             )
 
-        def mean_e(i, eng):
-            if eng == "S":
-                nc.scalar.activation(
-                    out=col(i, 24, 28), in_=col(i, 16, 20), func=ACT.Copy, scale=INV_V, accum_out=col(i, 9)
+        def mean_e(engine, i):
+            unused = stat(i, slice(24, 24 + SCRATCH))
+            if engine == "V":
+                nc.vector.tensor_scalar(
+                    out=unused, in0=stat(i, SUMS_E), scalar1=INV_V, scalar2=None, op0=ALU.mult, op1=ALU.add,
+                    accum_out=stat(i, MEAN_E),
                 )
-                return
-            nc.vector.tensor_scalar(
-                out=col(i, 24, 28), in0=col(i, 16, 20), scalar1=INV_V, scalar2=None, op0=ALU.mult, op1=ALU.add,
-                accum_out=col(i, 9),
-            )
+            else:
+                nc.scalar.activation(
+                    out=unused, in_=stat(i, SUMS_E), func=ACT.Copy, scale=INV_V, accum_out=stat(i, MEAN_E)
+                )
 
-        def mean_r(i, eng):
-            if eng == "S":
-                nc.scalar.activation(out=col(i, 10), in_=col(i, 20), func=ACT.Copy, scale=INV_V)
-                return
-            nc.vector.tensor_scalar(out=col(i, 10), in0=col(i, 20), scalar1=INV_V, scalar2=None, op0=ALU.mult)
-
-        def resid(i, which):
+        def subtract(i, which, mean):
             nc.vector.scalar_tensor_tensor(
-                out=work[i][:], in0=q_sb[which, i][:], scalar=col(i, 8 + which), in1=work[i][:],
+                out=rows[i][:], in0=q_in[which, i][:], scalar=stat(i, mean), in1=rows[i][:],
                 op0=ALU.mult, op1=ALU.subtract,
             )
 
-        def relu(i, which):
+        def relu(i, total):
             nc.scalar.activation(
-                out=work[i][:], in_=work[i][:], func=ACT.Relu, scale=-1.0, accum_out=col(i, 19 + which)
+                out=rows[i][:], in_=rows[i][:], func=ACT.Relu, scale=-1.0, accum_out=stat(i, total)
             )
 
-        def inv(i):
-            nc.vector.reciprocal(out=col(i, 11), in_=col(i, 21))
+        def mean_d1(engine, i):
+            if engine == "V":
+                nc.vector.tensor_scalar(
+                    out=stat(i, MEAN_D1), in0=stat(i, SUM_D1), scalar1=INV_V, scalar2=None, op0=ALU.mult
+                )
+            else:
+                nc.scalar.activation(out=stat(i, MEAN_D1), in_=stat(i, SUM_D1), func=ACT.Copy, scale=INV_V)
 
-        def gain_scale():
-            nc.vector.tensor_scalar(out=g_sb[:], in0=g_sb[:], scalar1=float(V), scalar2=None, op0=ALU.mult)
+        def invert_d2(i):
+            nc.vector.reciprocal(out=stat(i, INV_D2), in_=stat(i, SUM_D2))
 
-        def c_passes(i, z):
-            n = 4 // max(PARTS[i], 2)
+        def scale_gain():
+            nc.vector.tensor_scalar(out=gain[:], in0=gain[:], scalar1=float(V), scalar2=None, op0=ALU.mult)
+
+        c_rows, c_bank, c_woven, c_codes = {}, {}, {}, {}
+
+        def bank_passes(i, z):
+            n = V_PASSES // max(PARTS[i], 2)
             return range(z * n, (z + 1) * n)
 
-        def gain(i, hf):
-            if hf == 0:
-                c_sb[i] = stage.tile([P, V], BF16, name="c_sb", align_bytes=64)
-                c_group[i] = stage.tile([P, 4 * P, PACK], BF16, name="cg", align_bytes=64)
+        def apply_gain(i, part):
+            if part == 0:
+                c_rows[i] = stage.tile([P, V], BF16, name="c_rows", align_bytes=64)
+                c_woven[i] = stage.tile([P, V_PASSES * P, PACK], BF16, name="c_woven", align_bytes=64)
                 c_codes[i] = (
-                    stage.tile([P, 4, P], U32, name="cc", align_bytes=64),
-                    stage.tile([P, 4, P], U8, name="cs", align_bytes=64),
+                    stage.tile([P, V_PASSES, P], U32, name="c_code", align_bytes=64),
+                    stage.tile([P, V_PASSES, P], U8, name="c_scale", align_bytes=64),
                 )
             n = V // PARTS[i]
-            c = slice(hf * n, (hf + 1) * n)
+            cols = slice(part * n, (part + 1) * n)
             nc.vector.scalar_tensor_tensor(
-                out=c_sb[i][:, c], in0=work[i][:, c], scalar=col(i, 11), in1=g_sb[:, c], op0=ALU.mult, op1=ALU.mult
+                out=c_rows[i][:, cols], in0=rows[i][:, cols], scalar=stat(i, INV_D2), in1=gain[:, cols],
+                op0=ALU.mult, op1=ALU.mult,
             )
 
-        def c_quant(i, hf):
-            cd, sc = c_codes[i]
-            n = 4 // PARTS[i]
-            ks = slice(hf * n, (hf + 1) * n)
-            rs = slice(hf * n * P, (hf + 1) * n * P)
-            quant(
-                cd[:, ks, :].rearrange("p g r -> p (g r)"),
-                sc[:, ks, :].rearrange("p g r -> p (g r)"),
-                c_group[i][:, rs, :].rearrange("p r t -> p (r t)"),
+        def turn_c(i, z):
+            passes = bank_passes(i, z)
+            c_bank[i, z] = psum.tile([P, len(passes), 2, P], F32, name="turned", tag="turned", bufs=2)
+            turn(c_bank[i, z], c_rows[i][:].bitcast(F32), passes)
+
+        def lift_c(i, z):
+            passes = bank_passes(i, z)
+            lift(c_woven[i][:, P * passes[0] : P * (passes[-1] + 1), :], c_bank[i, z])
+
+        def quant_c(i, part):
+            codes, scales = c_codes[i]
+            n = V_PASSES // PARTS[i]
+            passes = slice(part * n, (part + 1) * n)
+            quantise(
+                codes[:, passes, :].rearrange("p g r -> p (g r)"),
+                scales[:, passes, :].rearrange("p g r -> p (g r)"),
+                c_woven[i][:, part * n * P : (part + 1) * n * P, :].rearrange("p r t -> p (r t)"),
             )
 
-        def mm2(i, hf, ks):
-            if (i, hf) not in acc:
-                acc[i, hf] = psum.tile([P, CH], F32, name=f"acc{hf}", tag=f"acc{hf}")
-            cd, sc = c_codes[i]
-            for k in ks:
-                ec, es = e_codes[k]
+        acc = {}
+
+        def second_matmul(i, half, passes):
+            if (i, half) not in acc:
+                acc[i, half] = psum.tile([P, BANK], F32, name=f"acc{half}", tag=f"acc{half}")
+            c_c, c_s = c_codes[i]
+            for k_pass in passes:
+                e_c, e_s = e_codes[k_pass]
                 nc.tensor.matmul_mx(
-                    out=acc[i, hf][:], lhsT=cd[:, k, :].bitcast(F8X4), lhsT_scale=sc[:, k, :],
-                    rhs=ec[:, hf, :].bitcast(F8X4), rhs_scale=es[:, hf, :], start=k == 0, stop=k == 3,
+                    out=acc[i, half][:],
+                    lhsT=c_c[:, k_pass, :].bitcast(F8X4),
+                    lhsT_scale=c_s[:, k_pass, :],
+                    rhs=e_c[:, half, :].bitcast(F8X4),
+                    rhs_scale=e_s[:, half, :],
+                    start=k_pass == 0,
+                    stop=k_pass == V_PASSES - 1,
                 )
 
-        def store(i, hf, eng):
-            t = stage.tile([P, CH], F32, name="res", bufs=3, align_bytes=64)
-            copy(eng, t[:], acc[i, hf][:])
-            nc.sync.dma_start(out=out[i * P : (i + 1) * P, hf * CH : (hf + 1) * CH], in_=t[:])
+        def one_pass(i, k_pass):
+            for half in range(HALVES):
+                second_matmul(i, half, (k_pass,))
 
-        def run(step):
-            kind, rest = step.split(":")
-            a = [int(x) for x in rest.split(".")]
-            eng = "V" if step in ON_VECTOR else "S"
-            if kind == "W":
-                widen(a[0], a[1], eng)
-            elif kind == "I":
-                w_inter(a[0], eng)
-            elif kind == "Q":
-                w_quant(a[0])
-            elif kind == "ht":
-                turn(("h", a[0]), h_sb[a[0]][:].bitcast(F32), range(2))
-            elif kind == "hc":
-                h_copy(a[0])
-            elif kind == "qh":
-                h_quant(a[0])
-            elif kind == "EP":
-                e_turn(a[0])
-            elif kind == "EI":
-                e_inter(a[0], eng)
-            elif kind == "EQ":
-                e_quant(a[0])
-            elif kind == "gs":
-                gain_scale()
-            elif kind == "mm":
-                mm1(a[0], a[1])
-            elif kind == "m":
-                rowmax(a[0], a[1])
-            elif kind == "n":
-                negmax(a[0])
-            elif kind == "e":
-                exp(a[0], a[1])
-            elif kind == "sa":
-                mean_e(a[0], eng)
-            elif kind == "ta":
-                resid(a[0], 1)
-            elif kind == "ra":
-                relu(a[0], 1)
-            elif kind == "sb":
-                mean_r(a[0], eng)
-            elif kind == "tb":
-                resid(a[0], 2)
-            elif kind == "rb":
-                relu(a[0], 2)
-            elif kind == "sc":
-                inv(a[0])
-            elif kind == "tc":
-                gain(a[0], a[1])
-            elif kind == "ct":
-                turn(("c", a[0], a[1]), c_sb[a[0]][:].bitcast(F32), c_passes(a[0], a[1]))
-            elif kind == "cc":
-                unturn(("c", a[0], a[1]), c_group[a[0]][:, P * c_passes(a[0], a[1])[0] : P * (c_passes(a[0], a[1])[-1] + 1), :])
-            elif kind == "qc":
-                c_quant(a[0], a[1])
-            elif kind == "oa":
-                for hf in range(2):
-                    mm2(a[0], hf, (a[1],))
-            elif kind == "o":
-                mm2(a[0], a[1], range(PARTS[a[0]] - 1, 4))
-            elif kind == "oc":
-                store(a[0], a[1], eng)
+        def last_passes(i, half):
+            second_matmul(i, half, range(PARTS[i] - 1, V_PASSES))
 
+        def store(engine, i, half):
+            result = stage.tile([P, BANK], F32, name="result", bufs=3, align_bytes=64)
+            copy(engine, result[:], acc[i, half][:])
+            nc.sync.dma_start(out=out[i * P : (i + 1) * P, half * BANK : (half + 1) * BANK], in_=result[:])
+
+        steps = {
+            "widenV": lambda u, pair: widen("V", u, pair),
+            "widenS": lambda u, pair: widen("S", u, pair),
+            "weave_w": weave_w,
+            "quant_w": quant_w,
+            "turn_h": turn_h,
+            "lift_h": lift_h,
+            "quant_h": quant_h,
+            "tensor_e": weave_e_on_tensor,
+            "bring_eV": lambda x: bring_e("V", x),
+            "bring_eS": lambda x: bring_e("S", x),
+            "quant_e": quant_e,
+            "mm1": first_matmul,
+            "max": row_max,
+            "negmax": neg_max,
+            "exp": exp,
+            "mean_eV": lambda i: mean_e("V", i),
+            "mean_eS": lambda i: mean_e("S", i),
+            "sub1": lambda i: subtract(i, 1, MEAN_E),
+            "relu1": lambda i: relu(i, SUM_D1),
+            "mean_dV": lambda i: mean_d1("V", i),
+            "mean_dS": lambda i: mean_d1("S", i),
+            "sub2": lambda i: subtract(i, 2, MEAN_D1),
+            "relu2": lambda i: relu(i, SUM_D2),
+            "invert": invert_d2,
+            "scale_gain": scale_gain,
+            "apply_gain": apply_gain,
+            "turn_c": turn_c,
+            "lift_c": lift_c,
+            "quant_c": quant_c,
+            "one_pass": one_pass,
+            "last_passes": last_passes,
+            "storeV": lambda i, half: store("V", i, half),
+            "storeS": lambda i, half: store("S", i, half),
+        }
         with tc.manual_schedule():
-            for step in ORDER:
-                run(step)
+            for step in " ".join(ORDER).split():
+                kind, arguments = step.split(":")
+                steps[kind](*[int(a) for a in arguments.split(".") if a])

from contextlib import ExitStack

import concourse.mybir as mybir
from concourse.masks import make_identity

F32 = mybir.dt.float32
BF16 = mybir.dt.bfloat16
U32 = mybir.dt.uint32
U8 = mybir.dt.uint8
F8 = mybir.dt.float8_e4m3fn
F8X4 = mybir.dt.float8_e4m3fn_x4
ACT = mybir.ActivationFunctionType
ALU = mybir.AluOpType
AX = mybir.AxisListType

N, D, V, E = 512, 1024, 2048, 1024
P = 128
PACK = 4
K_PASS = P * PACK
BANK = 512
D_PASSES = D // K_PASS
V_PASSES = V // K_PASS
CHUNKS = V // BANK
HALVES = E // BANK
PASS_WORDS = K_PASS // 2
RUN = 4
E_COLS = 256
BIG_SLOTS = 6
INV_V = 1.0 / V

FLOPS = 2 * N * D * V + 2 * N * V * E

UNITS = ((0, 0, 512), (1, 0, 512), (0, 512, 1024), (1, 512, 1024), (0, 1024, 2048), (1, 1024, 2048))
EARLY_UNITS = 2

PARTS = (1, 1, 1, 4)

MAXIMA = slice(0, 4)
NEG_MAX = slice(4, 5)
SUMS_E = slice(5, 9)
MEAN_E = slice(9, 10)
SUM_D1 = slice(10, 11)
MEAN_D1 = slice(11, 12)
SUM_D2 = slice(12, 13)
INV_D2 = slice(13, 14)
SCRATCH = 4

ORDER = (
    "widenV:0.0 widenV:0.1 widenS:1.1 weave_w:0 turn_h:0 widenV:2.1 widenS:2.0 quant_w:0 lift_h:0 widenV:3.0",
    "turn_h:1 widenS:1.0 weave_w:2 lift_h:1 weave_w:1 widenS:3.1 widenV:5.1 widenS:5.0 turn_h:2 weave_w:3",
    "turn_h:3 quant_h:0 widenS:4.0 quant_w:1 quant_w:2 mm1:0.0 quant_w:3 widenS:4.1 weave_w:5 mm1:0.1",
    "lift_h:2 tensor_e:2 weave_w:4 lift_h:3 bring_eS:1 tensor_e:3 quant_w:5 bring_eS:0 quant_w:4 max:0.0",
    "mm1:0.2 max:0.1 mm1:0.3 max:0.2 max:0.3 negmax:0",
    "scale_gain: exp:0.0 quant_h:1 exp:0.1 mm1:1.0 quant_e:0 exp:0.2 mm1:1.1 exp:0.3 mm1:1.2 max:1.0",
    "bring_eS:2 max:1.1 mm1:1.3 max:1.2 tensor_e:4 max:1.3 mean_eV:0 negmax:1 sub1:0 exp:1.0 exp:1.1 exp:1.2",
    "mm1:2.0 exp:1.3 mm1:2.1 max:2.0 bring_eS:3 mm1:2.2 mean_eV:1 max:2.1 mm1:2.3 sub1:1 relu1:0 tensor_e:5",
    "max:2.2 bring_eS:4 max:2.3 quant_e:1 mean_dS:0 relu1:1 tensor_e:6 negmax:2 sub2:0 exp:2.0 mean_dS:1",
    "exp:2.1 mm1:3.0 sub2:1 exp:2.2 mm1:3.1 exp:2.3 mm1:3.2 bring_eS:5 mm1:3.3 max:3.0 mean_eS:2 relu2:0",
    "tensor_e:7 quant_e:2 max:3.1 sub1:2 relu2:1 max:3.2 relu1:2 invert:0 invert:1 max:3.3 apply_gain:0.0",
    "bring_eS:6 negmax:3 apply_gain:1.0 bring_eS:7 exp:3.0 turn_c:0.0 mean_dS:2 exp:3.1 turn_c:0.1 sub2:2",
    "exp:3.2 lift_c:0.0 exp:3.3 turn_c:1.0 quant_e:3 lift_c:0.1 lift_c:1.0 turn_c:1.1 quant_c:0.0 mean_eS:3",
    "relu2:2 sub1:3 last_passes:0.0 last_passes:0.1 lift_c:1.1 invert:2 relu1:3 apply_gain:2.0 quant_c:1.0",
    "mean_dS:3 turn_c:2.0 storeS:0.1 sub2:3 storeS:0.0 turn_c:2.1 lift_c:2.0 last_passes:1.1 lift_c:2.1",
    "quant_c:2.0 relu2:3 last_passes:1.0 storeV:1.1 last_passes:2.1 storeV:1.0 invert:3 last_passes:2.0",
    "apply_gain:3.0 storeS:2.1 apply_gain:3.1 turn_c:3.0 apply_gain:3.2 storeS:2.0 turn_c:3.1 apply_gain:3.3",
    "lift_c:3.0 lift_c:3.1 turn_c:3.2 quant_c:3.0 quant_c:3.1 turn_c:3.3 lift_c:3.2 one_pass:3.0 lift_c:3.3",
    "quant_c:3.2 one_pass:3.1 quant_c:3.3 one_pass:3.2 last_passes:3.0 last_passes:3.1 storeV:3.0 storeS:3.1",
)


def tile_specinferrecursiveresidualverify_kernel(tc, h_t, w_bytes, w_scale, q1, q2, g, emb, out):
    nc = tc.nc
    with ExitStack() as ctx:
        keep = ctx.enter_context(tc.tile_pool(name="keep", bufs=1))
        stage = ctx.enter_context(tc.tile_pool(name="stage", bufs=2))
        psum = ctx.enter_context(tc.psum_pool(name="psum", bufs=1))

        warm = keep.tile([P, 1], F32, name="warm")
        nc.vector.memset(warm[:], 0.0)
        nc.scalar.activation(out=warm[:], in_=warm[:], func=ACT.Exp)
        ident = keep.tile([P, P], F32, name="ident")
        make_identity(nc, ident[:])
        ident16 = keep.tile([P, P], BF16, name="ident16")
        make_identity(nc, ident16[:])

        w_factor = keep.tile([P, D_PASSES, PACK], F32, name="w_factor")
        w_rows = w_bytes.rearrange("(g p t) n -> g p t n", p=P, t=PACK)
        emb_rows = emb.rearrange("(g p t) n -> g p t n", p=P, t=PACK)
        byte_plane, h_in, emb_in, q_in = {}, {}, {}, {}
        gain = keep.tile([P, V], BF16, name="gain")

        def load_w(u):
            k_pass, c0, c1 = UNITS[u]
            planes = 2 if u < EARLY_UNITS else PACK
            for t0 in range(0, PACK, planes):
                w_byte = keep.tile([P, planes, c1 - c0], U8, name=f"w_byte_{u}_{t0}", align_bytes=64)
                nc.sync.dma_start(out=w_byte[:], in_=w_rows[k_pass][:, t0 : t0 + planes, c0:c1])
                for t in range(planes):
                    byte_plane[u, t0 + t] = w_byte[:, t, :]

        def load_h(i):
            h_in[i] = keep.tile([P, D], BF16, name=f"h_{i}", align_bytes=64)
            nc.sync.dma_start(out=h_in[i][:], in_=h_t[i * P : (i + 1) * P, :])

        def load_q(i, which):
            q_in[which, i] = keep.tile([P, V], BF16, name=f"q{which}_{i}", align_bytes=64)
            nc.sync.dma_start(out=q_in[which, i][:], in_=(q1, q2)[which - 1][i * P : (i + 1) * P, :])

        def load_emb(k_pass):
            emb_in[k_pass] = keep.tile([P, PACK, E], BF16, name=f"emb_{k_pass}", align_bytes=64)
            nc.sync.dma_start(out=emb_in[k_pass][:], in_=emb_rows[k_pass])

        nc.sync.dma_start(out=w_factor[:], in_=w_scale.rearrange("(g p t) o -> p g (t o)", p=P, t=PACK))
        load_w(0)
        load_w(1)
        load_h(0)
        load_w(2)
        load_w(3)
        load_h(1)
        load_w(4)
        load_w(5)
        load_h(2)
        load_h(3)
        load_emb(0)
        load_q(0, 1)
        load_emb(1)
        load_q(0, 2)
        nc.sync.dma_start(out=gain[:], in_=g.partition_broadcast(P))
        load_q(1, 1)
        load_q(1, 2)
        load_emb(2)
        load_emb(3)
        for i in (2, 3):
            load_q(i, 1)
            load_q(i, 2)

        def copy(engine, dst, src):
            if engine == "V":
                nc.vector.tensor_copy(out=dst, in_=src)
            else:
                nc.scalar.copy(out=dst, in_=src)

        def weave(engine, dst, src):
            copy(engine, dst.rearrange("p (c i) t -> p c t i", i=RUN), src.rearrange("p t (c i) -> p c t i", i=RUN))

        def quantise(codes, scales, src):
            nc.vector.quantize_mx(out=codes.bitcast(F8X4), scales=scales, in_=src)

        def big(shape, dtype, name):
            return stage.tile(shape, dtype, name=name, tag="big", bufs=BIG_SLOTS, align_bytes=64)

        def turn(bank, words, passes):
            for b, k_pass in enumerate(passes):
                for u in range(2):
                    every_second = slice(PASS_WORDS * k_pass + u, PASS_WORDS * (k_pass + 1), 2)
                    nc.tensor.transpose(bank[:, b, u, :], words[:, every_second], ident[:])

        def lift(dst, bank):
            nc.scalar.copy(
                out=dst.rearrange("p r t -> p (r t)").bitcast(F32).rearrange("p (g r u) -> p g r u", r=P, u=2),
                in_=bank[:].rearrange("p g u r -> p g r u"),
            )

        w_planes, w_woven, w_codes = {}, {}, {}

        def widen(engine, u, pair):
            k_pass, c0, c1 = UNITS[u]
            if u not in w_planes:
                w_planes[u] = big([P, PACK, c1 - c0], BF16, "w_planes")
            for t in (2 * pair, 2 * pair + 1):
                src = byte_plane[u, t].bitcast(F8)
                factor = w_factor[:, k_pass, t : t + 1]
                if engine == "V":
                    nc.vector.tensor_scalar(
                        out=w_planes[u][:, t, :], in0=src, scalar1=factor, scalar2=None, op0=ALU.mult
                    )
                else:
                    nc.scalar.activation(out=w_planes[u][:, t, :], in_=src, func=ACT.Copy, scale=factor)

        def weave_w(u):
            k_pass, c0, c1 = UNITS[u]
            w_woven[u] = big([P, c1 - c0, PACK], BF16, "w_woven")
            weave("V", w_woven[u][:], w_planes[u][:])

        def quant_w(u):
            k_pass, c0, c1 = UNITS[u]
            codes = keep.tile([P, c1 - c0], U32, name=f"w_codes_{u}", align_bytes=64)
            scales = keep.tile([P, c1 - c0], U8, name=f"w_scales_{u}", align_bytes=64)
            quantise(codes[:], scales[:], w_woven[u][:].rearrange("p n t -> p (n t)"))
            for c in range(c0, c1, BANK):
                cols = slice(c - c0, c - c0 + BANK)
                w_codes[k_pass, c // BANK] = (codes[:, cols], scales[:, cols])

        h_bank, h_woven, h_codes = {}, {}, {}

        def turn_h(i):
            h_bank[i] = psum.tile([P, D_PASSES, 2, P], F32, name="turned", tag="turned", bufs=2)
            turn(h_bank[i], h_in[i][:].bitcast(F32), range(D_PASSES))

        def lift_h(i):
            pair = i // 2
            if i % 2 == 0:
                h_woven[pair] = stage.tile([P, 2, D_PASSES * P, PACK], BF16, name="h_woven", align_bytes=64)
            lift(h_woven[pair][:, i % 2, :, :], h_bank[i])

        def quant_h(pair):
            codes = keep.tile([P, 2, D_PASSES, P], U32, name=f"h_codes_{pair}", align_bytes=64)
            scales = keep.tile([P, 2, D_PASSES, P], U8, name=f"h_scales_{pair}", align_bytes=64)
            quantise(
                codes[:].rearrange("p a g r -> p (a g r)"),
                scales[:].rearrange("p a g r -> p (a g r)"),
                h_woven[pair][:].rearrange("p a r t -> p (a r t)"),
            )
            for a in range(2):
                h_codes[2 * pair + a] = (codes[:, a], scales[:, a])

        e_banks, e_woven, e_codes = {}, {}, {}

        def weave_e_on_tensor(x):
            k_pass, half = divmod(x, 2)
            e_banks[x] = []
            for z in range(BANK // E_COLS):
                if x % 2 == 0:
                    bank = psum.tile([P, E_COLS, PACK], BF16, name=f"e_bank{z}", tag=f"acc{z}")
                else:
                    bank = psum.tile([P, E_COLS, PACK], BF16, name=f"e_bank{z}", tag="turned", bufs=2)
                for y in range(E_COLS // P):
                    c0 = half * BANK + z * E_COLS + y * P
                    nc.tensor.matmul(
                        bank[:, y * P : (y + 1) * P, :].rearrange("p (c i) t -> p c t i", i=RUN),
                        lhsT=ident16[:],
                        rhs=emb_in[k_pass][:, :, c0 : c0 + P].rearrange("p t (c i) -> p c t i", i=RUN),
                        start=True,
                        stop=True,
                    )
                e_banks[x].append(bank)

        def bring_e(engine, x):
            k_pass, half = divmod(x, 2)
            if k_pass not in e_woven:
                e_woven[k_pass] = stage.tile([P, HALVES, BANK, PACK], BF16, name="e_woven", align_bytes=64)
            if x in e_banks:
                for z in range(BANK // E_COLS):
                    copy(engine, e_woven[k_pass][:, half, z * E_COLS : (z + 1) * E_COLS, :], e_banks[x][z][:])
            else:
                weave(engine, e_woven[k_pass][:, half, :, :], emb_in[k_pass][:, :, half * BANK : (half + 1) * BANK])

        def quant_e(k_pass):
            codes = keep.tile([P, HALVES, BANK], U32, name=f"e_codes_{k_pass}", align_bytes=64)
            scales = keep.tile([P, HALVES, BANK], U8, name=f"e_scales_{k_pass}", align_bytes=64)
            quantise(
                codes[:].rearrange("p h n -> p (h n)"),
                scales[:].rearrange("p h n -> p (h n)"),
                e_woven[k_pass][:].rearrange("p h n t -> p (h n t)"),
            )
            e_codes[k_pass] = (codes, scales)

        lt, rows, stats = {}, {}, {}

        def stat(i, cols):
            if i not in stats:
                stats[i] = keep.tile([P, 32], F32, name=f"stats_{i}")
            return stats[i][:, cols]

        def first_matmul(i, j):
            lt[i, j] = psum.tile([P, BANK], F32, name=f"lt{j}", tag=f"lt{j}")
            h_c, h_s = h_codes[i]
            for k_pass in range(D_PASSES):
                w_c, w_s = w_codes[k_pass, j]
                nc.tensor.matmul_mx(
                    out=lt[i, j][:],
                    lhsT=h_c[:, k_pass, :].bitcast(F8X4),
                    lhsT_scale=h_s[:, k_pass, :],
                    rhs=w_c.bitcast(F8X4),
                    rhs_scale=w_s,
                    start=k_pass == 0,
                    stop=k_pass == D_PASSES - 1,
                )

        def row_max(i, j):
            nc.vector.tensor_reduce(out=stat(i, MAXIMA)[:, j : j + 1], in_=lt[i, j][:], axis=AX.X, op=ALU.max)

        def neg_max(i):
            nc.vector.tensor_reduce(
                out=stat(i, NEG_MAX), in_=stat(i, MAXIMA), axis=AX.X, op=ALU.max, negate=True
            )

        def exp(i, j):
            if j == 0:
                rows[i] = big([P, V], F32, "rows")
            nc.scalar.activation(
                out=rows[i][:, j * BANK : (j + 1) * BANK],
                in_=lt[i, j][:],
                func=ACT.Exp,
                bias=stat(i, NEG_MAX),
                scale=1.0,
                accum_out=stat(i, SUMS_E)[:, j : j + 1],
            )

        def mean_e(engine, i):
            unused = stat(i, slice(24, 24 + SCRATCH))
            if engine == "V":
                nc.vector.tensor_scalar(
                    out=unused, in0=stat(i, SUMS_E), scalar1=INV_V, scalar2=None, op0=ALU.mult, op1=ALU.add,
                    accum_out=stat(i, MEAN_E),
                )
            else:
                nc.scalar.activation(
                    out=unused, in_=stat(i, SUMS_E), func=ACT.Copy, scale=INV_V, accum_out=stat(i, MEAN_E)
                )

        def subtract(i, which, mean):
            nc.vector.scalar_tensor_tensor(
                out=rows[i][:], in0=q_in[which, i][:], scalar=stat(i, mean), in1=rows[i][:],
                op0=ALU.mult, op1=ALU.subtract,
            )

        def relu(i, total):
            nc.scalar.activation(
                out=rows[i][:], in_=rows[i][:], func=ACT.Relu, scale=-1.0, accum_out=stat(i, total)
            )

        def mean_d1(engine, i):
            if engine == "V":
                nc.vector.tensor_scalar(
                    out=stat(i, MEAN_D1), in0=stat(i, SUM_D1), scalar1=INV_V, scalar2=None, op0=ALU.mult
                )
            else:
                nc.scalar.activation(out=stat(i, MEAN_D1), in_=stat(i, SUM_D1), func=ACT.Copy, scale=INV_V)

        def invert_d2(i):
            nc.vector.reciprocal(out=stat(i, INV_D2), in_=stat(i, SUM_D2))

        def scale_gain():
            nc.vector.tensor_scalar(out=gain[:], in0=gain[:], scalar1=float(V), scalar2=None, op0=ALU.mult)

        c_rows, c_bank, c_woven, c_codes = {}, {}, {}, {}

        def bank_passes(i, z):
            n = V_PASSES // max(PARTS[i], 2)
            return range(z * n, (z + 1) * n)

        def apply_gain(i, part):
            if part == 0:
                c_rows[i] = stage.tile([P, V], BF16, name="c_rows", align_bytes=64)
                c_woven[i] = stage.tile([P, V_PASSES * P, PACK], BF16, name="c_woven", align_bytes=64)
                c_codes[i] = (
                    stage.tile([P, V_PASSES, P], U32, name="c_code", align_bytes=64),
                    stage.tile([P, V_PASSES, P], U8, name="c_scale", align_bytes=64),
                )
            n = V // PARTS[i]
            cols = slice(part * n, (part + 1) * n)
            nc.vector.scalar_tensor_tensor(
                out=c_rows[i][:, cols], in0=rows[i][:, cols], scalar=stat(i, INV_D2), in1=gain[:, cols],
                op0=ALU.mult, op1=ALU.mult,
            )

        def turn_c(i, z):
            passes = bank_passes(i, z)
            c_bank[i, z] = psum.tile([P, len(passes), 2, P], F32, name="turned", tag="turned", bufs=2)
            turn(c_bank[i, z], c_rows[i][:].bitcast(F32), passes)

        def lift_c(i, z):
            passes = bank_passes(i, z)
            lift(c_woven[i][:, P * passes[0] : P * (passes[-1] + 1), :], c_bank[i, z])

        def quant_c(i, part):
            codes, scales = c_codes[i]
            n = V_PASSES // PARTS[i]
            passes = slice(part * n, (part + 1) * n)
            quantise(
                codes[:, passes, :].rearrange("p g r -> p (g r)"),
                scales[:, passes, :].rearrange("p g r -> p (g r)"),
                c_woven[i][:, part * n * P : (part + 1) * n * P, :].rearrange("p r t -> p (r t)"),
            )

        acc = {}

        def second_matmul(i, half, passes):
            if (i, half) not in acc:
                acc[i, half] = psum.tile([P, BANK], F32, name=f"acc{half}", tag=f"acc{half}")
            c_c, c_s = c_codes[i]
            for k_pass in passes:
                e_c, e_s = e_codes[k_pass]
                nc.tensor.matmul_mx(
                    out=acc[i, half][:],
                    lhsT=c_c[:, k_pass, :].bitcast(F8X4),
                    lhsT_scale=c_s[:, k_pass, :],
                    rhs=e_c[:, half, :].bitcast(F8X4),
                    rhs_scale=e_s[:, half, :],
                    start=k_pass == 0,
                    stop=k_pass == V_PASSES - 1,
                )

        def one_pass(i, k_pass):
            for half in range(HALVES):
                second_matmul(i, half, (k_pass,))

        def last_passes(i, half):
            second_matmul(i, half, range(PARTS[i] - 1, V_PASSES))

        def store(engine, i, half):
            result = stage.tile([P, BANK], F32, name="result", bufs=3, align_bytes=64)
            copy(engine, result[:], acc[i, half][:])
            nc.sync.dma_start(out=out[i * P : (i + 1) * P, half * BANK : (half + 1) * BANK], in_=result[:])

        steps = {
            "widenV": lambda u, pair: widen("V", u, pair),
            "widenS": lambda u, pair: widen("S", u, pair),
            "weave_w": weave_w,
            "quant_w": quant_w,
            "turn_h": turn_h,
            "lift_h": lift_h,
            "quant_h": quant_h,
            "tensor_e": weave_e_on_tensor,
            "bring_eV": lambda x: bring_e("V", x),
            "bring_eS": lambda x: bring_e("S", x),
            "quant_e": quant_e,
            "mm1": first_matmul,
            "max": row_max,
            "negmax": neg_max,
            "exp": exp,
            "mean_eV": lambda i: mean_e("V", i),
            "mean_eS": lambda i: mean_e("S", i),
            "sub1": lambda i: subtract(i, 1, MEAN_E),
            "relu1": lambda i: relu(i, SUM_D1),
            "mean_dV": lambda i: mean_d1("V", i),
            "mean_dS": lambda i: mean_d1("S", i),
            "sub2": lambda i: subtract(i, 2, MEAN_D1),
            "relu2": lambda i: relu(i, SUM_D2),
            "invert": invert_d2,
            "scale_gain": scale_gain,
            "apply_gain": apply_gain,
            "turn_c": turn_c,
            "lift_c": lift_c,
            "quant_c": quant_c,
            "one_pass": one_pass,
            "last_passes": last_passes,
            "storeV": lambda i, half: store("V", i, half),
            "storeS": lambda i, half: store("S", i, half),
        }
        with tc.manual_schedule():
            for step in " ".join(ORDER).split():
                kind, arguments = step.split(":")
                steps[kind](*[int(a) for a in arguments.split(".") if a])
